import numpy as np, ml_dtypes
CORES = [3,11,19,27,35,43,51,59]
N = 8
import mx_ref
BF = ml_dtypes.bfloat16
def entries(a):
    return np.ascontiguousarray(a.T).reshape(-1)
def table(e):
    return np.ascontiguousarray(np.reshape(e, (-1, 16)).T).astype(np.int32)
def cut(t, i, w=512):
    return t[:, w * i:w * i + w]
def decode(q):
    o = []
    for b in range(4):
        e = np.zeros((128, 128, 4), np.float32); e[np.arange(128), np.arange(128), b] = 1
        o.append(mx_ref.matmul(mx_ref.quantize(e.reshape(128, 512).astype(BF)), q))
    return np.stack(o, axis=2).reshape(128, -1)
def f(rng, *shape):
    return mx_ref.flush((rng.standard_normal(shape, dtype=np.float32) * np.exp2(rng.integers(-2, 3, shape[:-1] + (1,)))).astype(BF))
def wide(rng, *shape, cols=0):
    v = rng.standard_normal(shape, dtype=np.float32) * np.exp2(rng.integers(-12, 13, shape)).astype(np.float32)
    if cols: v *= np.repeat(np.exp2(rng.integers(-cols, cols + 1, shape[:-2] + (1, shape[-1] // 4))) * (rng.random(shape[:-2] + (1, shape[-1] // 4)) > 0.0625), 4, axis=-1).astype(np.float32)
    return mx_ref.flush(v.astype(BF))
T, K, O = 256, 256, 2
HA = (1237, 1811, 947, 1543, 2017, 733, 1409, 1699)
HB = (40503, 12289, 58111, 3571, 27644, 61007, 19211, 50021)
def setup_inputs(rng):
    return {"tb": f(rng, N, 128, 4 * K), "ids": np.stack([table(rng.integers(0, 4096, T)) for r in range(N)]), "w": f(rng, N, 128, 512 * O)}
def setup_inputs_alike(rng):
    d = setup_inputs(rng); e = rng.integers(0, 4096, T)
    d["ids"] = np.stack([table(e) for r in range(N)]); return d
def setup_inputs_ends(rng):
    d = setup_inputs(rng); o = []
    for r in range(N):
        e = rng.choice([0, 4095], T); e[rng.permutation(T)[:2]] = [0, 4095]
        o.append(table(e))
    d["ids"] = np.stack(o); return d
def setup_inputs_order(rng):
    d = setup_inputs(rng); t = rng.standard_normal((N, 128, 4 * K), dtype=np.float32)
    one = rng.permutation(np.concatenate([np.arange(N), rng.integers(0, N, 16 - N)]))
    for g in range(16):
        p = int(one[g]); o = int(rng.choice([q for q in range(N) if abs(q - p) >= 2]))
        size = np.float32(2.0 ** int(rng.integers(0, 3)))
        X = np.tile(rng.choice([-1, 1], (8, 4)).astype(np.float32) * size, (1, K))
        v = t[:, 8 * g:8 * g + 8]; v *= size * np.float32(2.0 ** -14)
        v[min(p, o)] = X; v[max(p, o)] = -X
    d["tb"] = mx_ref.flush(t.astype(BF)); return d
def setup_inputs_same(rng):
    d = setup_inputs(rng)
    d["ids"] = np.stack([table(np.full(T, rng.integers(0, 4096))) for r in range(N)]); return d
def setup_inputs_spread(rng):
    d = setup_inputs(rng); d["tb"] = wide(rng, N, 128, 4 * K, cols=8); return d
def check_inputs(d):
    b = []
    for r in range(N):
        e = entries(d["ids"][r])
        if e.min() < 0 or e.max() > 4095: b.append("ids")
    return b
def address(q, e):
    return ((e * HA[q] + HB[q]) >> 5) & (K - 1)
def reference(tb, ids, w):
    d = [decode(mx_ref.quantize(tb[q])).reshape(128, -1, 4) for q in range(N)]
    y = np.zeros((N, 128, O * T), np.float32)
    for r in range(N):
        e = entries(ids[r])
        v = d[0][:, address(0, e)]
        for q in range(1, N): v = v + d[q][:, address(q, e)]
        V = mx_ref.quantize(np.ascontiguousarray(v.reshape(128, -1)).astype(BF))
        for o in range(O): y[r][:, T * o:T * o + T] = mx_ref.matmul(mx_ref.quantize(np.ascontiguousarray(cut(w[r], o))), V)
    return {"y": y}

@@ -1,0 +1,361 @@
+from concourse.bass import DstId, RemoteDMATransfer
+from concourse.mybir import dt, AluOpType, ActivationFunctionType
+
+N, TOK, K, O = 8, 256, 256, 2
+H = TOK // 2
+HA = (1237, 1811, 947, 1543, 2017, 733, 1409, 1699)
+HB = (40503, 12289, 58111, 3571, 27644, 61007, 19211, 50021)
+SHARE = (2, 3, 2, 3, 2, 3, 2)
+SLOTS = 2 * (N - 1)
+LH = H // 16
+WIN = 4 * K - 3
+
+SCRATCH = {
+    "ids8": ("sbuf", [128, 16], "int32"),
+    "ox": ("sbuf", [128, 16], "int32"),
+    "oy": ("sbuf", [128, 16], "int32"),
+    "oo": ("sbuf", [128, 16], "uint16"),
+    "lst": ("sbuf", [128, LH * SLOTS], "int32"),
+    "lx": ("sbuf", [128, LH * SLOTS], "int32"),
+    "ly": ("sbuf", [128, LH * SLOTS], "int32"),
+    "lo": ("sbuf", [128, LH * SLOTS], "uint16"),
+    "ws": ("sbuf", [128, 512 * O], "bfloat16"),
+    "ones": ("sbuf", [128, 520], "bfloat16"),
+    "ez": ("sbuf", [128, 520], "bfloat16"),
+    "ec": ("sbuf", [128, 512], "float8_e4m3fn_x4"),
+    "es": ("sbuf", [128, 512], "uint8"),
+    "wc": ("sbuf", [128, 128 * O], "float8_e4m3fn_x4"),
+    "wp": ("sbuf", [128, 128 * O], "uint8"),
+    "rc": ("sbuf", [128, N * TOK], "float8_e4m3fn_x4"),
+    "rs": ("sbuf", [128, N * TOK], "uint8"),
+    "hc": ("sbuf", [128, 4 * TOK], "float8_e4m3fn_x4"),
+    "hs": ("sbuf", [128, 4 * TOK], "uint8"),
+    "vt0": ("sbuf", [128, 4 * H], "bfloat16"),
+    "vt1": ("sbuf", [128, 4 * H], "bfloat16"),
+    "vc": ("sbuf", [128, TOK], "float8_e4m3fn_x4"),
+    "vs": ("sbuf", [128, TOK], "uint8"),
+    "yo": ("sbuf", [128, O * TOK], "float32"),
+    "ps": ("psum", [128, 512 * 8], "float32"),
+}
+for _i in range(4):
+    SCRATCH["tb%d" % _i] = ("sbuf", [128, 4 * K], "bfloat16")
+for _i in range(N):
+    SCRATCH["h%d" % _i] = ("sbuf", [128, 4 * TOK], "bfloat16")
+for _i in range(N - 1):
+    SCRATCH["qc%d" % _i] = ("sbuf", [128, TOK], "float8_e4m3fn_x4")
+    SCRATCH["qs%d" % _i] = ("sbuf", [128, TOK], "uint8")
+
+SEMAPHORES = ["idl", "tbl", "wl", "v", "s", "t", "ga", "lists0", "lists1", "lists2", "sent", "yd"]
+SEMAPHORES += ["hcode%d" % i for i in range(8)] + ["hplane%d" % i for i in range(8)]
+SEMAPHORES += ["arr%d_%d" % (h, q) for h in range(2) for q in range(N)]
+
+
+def bits(m):
+    return bin(m).count("1")
+
+
+def as_mask(engines):
+    return sum(1 << e for e in engines)
+
+
+def plan(core, T, topo):
+    ch = topo.chip(core)
+    r = T.rank_of(core)
+    ring = [(r + k) % N for k in range(1, N)]
+    mate = [d for d in ring if topo.mates(ch, topo.chip(T.cores[d]))]
+    plane = [d for d in ring if topo.same_plane(ch, topo.chip(T.cores[d]))]
+    far = [d for d in ring if d not in mate and d not in plane]
+    help_ = [c for c in topo.cores_of(core)
+             if topo.die(c) != topo.die(core) and all(topo.may_write(c, T.cores[d]) for d in far)]
+    off = {e for d in ring for e in topo.engines(core, T.cores[d])}
+    helper = {d: help_[i % len(help_)] for i, d in enumerate(far)}
+    D = plane + mate
+    first = far[:2] + D + far[2:]
+    second = far[2:] + far[:2] + D
+    slot = {(d, 0): i for i, d in enumerate(first)}
+    slot.update({(d, 1): N - 1 + i for i, d in enumerate(second)})
+    shape = [[(far[0], 0), (far[1], 0)], [(D[0], 0), (D[1], 0)], [(far[2], None)], [(D[2], 0), (D[3], 0)],
+             [(far[0], 1), (far[1], 1)], [(D[0], 1), (D[1], 1)], [(D[2], 1), (D[3], 1)]]
+    used = {c: [0, 0] for c in help_}
+    units = []
+    for u in shape:
+        pieces = []
+        for i, (d, half) in enumerate(u):
+            n = TOK if half is None else H
+            via = helper.get(d)
+            if via is None:
+                e = topo.engines(core, T.cores[d])
+            else:
+                e = [x for x in topo.engines(core, via) if x not in off]
+            w = len(e) // len(u)
+            p = {"to": d, "half": half, "slot": slot[(d, half or 0)], "col": i * H, "n": n, "via": via, "mask": as_mask(e[i * w:i * w + w])}
+            if via is not None:
+                p["place"], p["at"] = used[via]
+                used[via] = [p["place"] + 1, p["at"] + n]
+            pieces.append(p)
+        units.append(pieces)
+    return units, slot
+
+
+def column(q, half):
+    return TOK * q + H * (half or 0)
+
+
+def rank_program(g, core, T, topo):
+    rank = T.rank_of(core)
+    if rank is None:
+        helper_program(g, core, T, topo)
+        return
+    owner_program(g, core, rank, T, topo)
+
+
+def helper_program(g, core, T, topo):
+    total = 0
+    for src in T.cores:
+        if topo.chip(src) != topo.chip(core):
+            continue
+        q = T.rank_of(src)
+        for p in [p for u in plan(src, T, topo)[0] for p in u if p["via"] == core]:
+            dst = T.cores[p["to"]]
+            rid, pid, _ = topo.addr(dst)
+            n_in = bits(p["mask"])
+            m = topo.mask(core, dst)
+            arr = T.sem["arr%d_%d" % (p["half"] or 0, q)]
+            a, b, n = column(q, p["half"]), p["at"], p["n"]
+            g.wait_ge(T.sem["hcode%d" % p["place"]], n_in)
+            g.remote_dma(T.rc[:, a:a + n].bitcast(dt.uint8), T.hc[:, b:b + n].bitcast(dt.uint8), arr, T.sem.sent, pid, rid, m)
+            g.wait_ge(T.sem["hplane%d" % p["place"]], n_in)
+            g.remote_dma(T.rs[:, a:a + n], T.hs[:, b:b + n], arr, T.sem.sent, pid, rid, m)
+            total += 2 * bits(m)
+    if total:
+        g.wait_ge(T.sem.sent, total)
+
+
+def arrival(q, r, half, T, topo):
+    for i, u in enumerate(plan(T.cores[q], T, topo)[0]):
+        for p in u:
+            if p["to"] == r and p["half"] in (half, None):
+                if p["via"] is None:
+                    m, hops = p["mask"], 2
+                else:
+                    m, hops = topo.mask(p["via"], T.cores[r]), 4
+                return i + hops, "arr%d_%d" % (p["half"] or 0, q), 2 * bits(m)
+
+
+def chain(r, half, T, topo):
+    return sorted([0, 1], key=lambda q: 0 if q == r else arrival(q, r, half, T, topo)[0]) + list(range(2, N))
+
+
+def owner_program(g, core, r, T, topo):
+    vec, sca, ten, syn = g.vector, g.scalar, g.tensor, g.sync
+    A = AluOpType
+    COPY = ActivationFunctionType.Copy
+    cnt = {"v": 0, "s": 0, "t": 0}
+    seen = {}
+
+    def done(name, ins):
+        ins.then_inc(T.sem[name], 1)
+        cnt[name] += 1
+        return cnt[name]
+
+    def need(queue, me, name, val):
+        if val > seen.get((me, name), 0):
+            queue.wait_ge(T.sem[name], val)
+            seen[(me, name)] = val
+
+    units, _ = plan(core, T, topo)
+    others = [d for d in range(N) if d != r]
+
+    for i in range(8):
+        (syn if i < 4 else sca).dma_start(T.ids8[16 * i:16 * i + 16, :], T.ids[:, :]).then_inc(T.sem.idl, 16)
+    syn.dma_start(T.tb0[:, :], T.tb[:, :]).then_inc(T.sem.tbl, 16)
+
+    n_ones = done("v", vec.memset(T.ones[:, :], 1.0))
+    g.wait_ge(T.sem.v, n_ones)
+    g.affine_select(T.ez[:, :], T.ones[:, :], [[1, 520]], A.is_equal, 0.0, -4, -4).then_inc(T.sem.ga, 1)
+
+    GROUPS = ((0, 4), (4, N - 1), (N - 1, SLOTS))
+    g.wait_ge(T.sem.idl, 128)
+    sent = 0
+    mine = {d: plan(T.cores[d], T, topo)[1] for d in others}
+    for k, (lo_, hi_) in enumerate(GROUPS):
+        ids_, dsts, mask, half = [], [], None, k // 2
+        for d in sorted(others, key=lambda x: mine[x][(r, half)]):
+            s = mine[d][(r, half)]
+            if not lo_ <= s < hi_:
+                continue
+            dst = T.cores[d]
+            rid, pid, _ = topo.addr(dst)
+            ids_.append(DstId(rid=rid, pnc=pid))
+            dsts.append(T.lst[:, LH * s:LH * s + LH])
+            m = topo.mask(core, dst)
+            mask = m if mask is None else mask & m
+        sent += bits(mask)
+        g.remote_dma_fused([RemoteDMATransfer(dst_ids=ids_, dma_engine_mask=mask, remote_sem=T.sem["lists%d" % k], srcs=[T.ids8[:, LH * half:LH * half + LH]], dsts=dsts)], local_sem=T.sem.sent)
+    each = bits(mask)
+    state = {"sent": sent}
+
+    vec.wait_ge(T.sem.ga, 1)
+    for b in range(4):
+        n_e = done("v", vec.quantize_mx(T.ec[:, 128 * b:128 * b + 128], T.es[:, 128 * b:128 * b + 128], T.ez[:, 4 - b:4 - b + 512]))
+
+    def hashes(src, x, y, off, a, b):
+        n = done("v", vec.tensor_scalar(x[:, a:b], src[:, a:b], HA[r], HB[r], A.mult, A.add))
+        need(vec, "v", "v", n)
+        n = done("v", vec.tensor_scalar(y[:, a:b], x[:, a:b], 3, 4 * (K - 1), A.arith_shift_right, A.bitwise_and))
+        need(vec, "v", "v", n)
+        return done("v", vec.tensor_copy(off[:, a:b], y[:, a:b]))
+
+    def pick(eng, me, h, off, t, n_off):
+        need(eng, me, "v", n_off)
+        if t:
+            need(eng, me, moved[t][0], moved[t][1])
+        o, i = h[:, t:4 * TOK:4], T["tb%d" % t][:, 0:WIN].indirect(off)
+        return done(me, sca.activation(o, i, COPY) if me == "s" else vec.tensor_copy(o, i))
+
+    vec.wait_ge(T.sem.idl, 128)
+    n_oo = hashes(T.ids8, T.ox, T.oy, T.oo, 0, 16)
+    own = {"h": T["h%d" % (N - 1)], "c": T.rc[:, TOK * r:TOK * r + TOK], "p": T.rs[:, TOK * r:TOK * r + TOK]}
+    moved = {}
+    sca.wait_ge(T.sem.tbl, 16)
+    moved[1] = ("s", done("s", sca.activation(T.tb1[:, 0:WIN], T.tb0[:, 1:1 + WIN], COPY)))
+    vec.wait_ge(T.sem.tbl, 16)
+    for t in (2, 3):
+        moved[t] = ("v", done("v", vec.tensor_copy(T["tb%d" % t][:, 0:WIN], T.tb0[:, t:t + WIN])))
+    for t in (0, 1):
+        own["s"] = pick(sca, "s", own["h"], T.oo[:, 0:16], t, n_oo)
+    for t in (2, 3):
+        own["v"] = pick(vec, "v", own["h"], T.oo[:, 0:16], t, n_oo)
+
+    def pack(u):
+        need(vec, "v", "v", u["v"])
+        need(vec, "v", "s", u["s"])
+        return done("v", vec.quantize_mx(u["c"], u["p"], u["h"][:, 0:4 * TOK]))
+
+    def pack_and_send(u):
+        n = pack(u)
+        if "pieces" not in u:
+            u["n"] = n
+            return
+        g.wait_ge(T.sem.v, n)
+        codes, planes = [], []
+        for p in u["pieces"]:
+            a, c, w = column(r, p["half"]), p["col"], p["n"]
+            if p["via"] is None:
+                dst, oc, op = T.cores[p["to"]], T.rc[:, a:a + w], T.rs[:, a:a + w]
+                sc = sp = T.sem["arr%d_%d" % (p["half"] or 0, r)]
+            else:
+                b = p["at"]
+                dst, oc, op = p["via"], T.hc[:, b:b + w], T.hs[:, b:b + w]
+                sc, sp = T.sem["hcode%d" % p["place"]], T.sem["hplane%d" % p["place"]]
+            rid, pid, _ = topo.addr(dst)
+            to = [DstId(rid=rid, pnc=pid)]
+            codes.append(RemoteDMATransfer(dst_ids=to, dma_engine_mask=p["mask"], remote_sem=sc, srcs=[u["c"][c:c + w].bitcast(dt.uint8)] if False else [u["qc"][:, c:c + w].bitcast(dt.uint8)], dsts=[oc.bitcast(dt.uint8)]))
+            planes.append(RemoteDMATransfer(dst_ids=to, dma_engine_mask=p["mask"], remote_sem=sp, srcs=[u["qs"][:, c:c + w]], dsts=[op]))
+            state["sent"] += 2 * bits(p["mask"])
+        g.remote_dma_fused(codes, local_sem=T.sem.sent)
+        g.remote_dma_fused(planes, local_sem=T.sem.sent)
+
+    n_of = {}
+
+    def listed(ks):
+        for k in ks:
+            vec.wait_ge(T.sem["lists%d" % k], each * (GROUPS[k][1] - GROUPS[k][0]))
+        a, b = GROUPS[ks[0]][0], GROUPS[ks[-1]][1]
+        n = hashes(T.lst, T.lx, T.ly, T.lo, LH * a, LH * b)
+        for i in range(a, b):
+            n_of[i] = n
+
+    listed([0])
+    before = own
+    for i, pieces in enumerate(units):
+        u = {"h": T["h%d" % i], "qc": T["qc%d" % i], "qs": T["qs%d" % i], "c": T["qc%d" % i][:, 0:TOK], "p": T["qs%d" % i][:, 0:TOK], "pieces": pieces}
+        s = pieces[0]["slot"]
+        off = T.lo[:, LH * s:LH * s + 2 * LH]
+        for t in range(SHARE[i]):
+            u["s"] = pick(sca, "s", u["h"], off, t, n_of[s + 1])
+        for t in range(SHARE[i], 4):
+            u["v"] = pick(vec, "v", u["h"], off, t, n_of[s + 1])
+            if before is not None:
+                pack_and_send(before)
+                before = None
+        before = u
+        if i == 1:
+            listed([1, 2])
+    pack_and_send(before)
+
+    syn.wait_ge(T.sem.lists0, each * GROUPS[0][1])
+    syn.dma_start(T.ws[:, :], T.w[:, :]).then_inc(T.sem.wl, 16)
+    vec.wait_ge(T.sem.wl, 16)
+    n_w = done("v", vec.quantize_mx(T.wc[:, 0:128 * O], T.wp[:, 0:128 * O], T.ws[:, 0:512 * O]))
+
+    need(ten, "t", "v", n_e)
+    waited = {}
+
+    def add(half, k, q):
+        if q == r:
+            need(ten, "t", "v", own["n"])
+        else:
+            _, sem, n = arrival(q, r, half, T, topo)
+            if sem not in waited:
+                ten.wait_ge(T.sem[sem], n)
+                waited[sem] = n
+        a, n_t = column(q, half), []
+        for b in range(4):
+            c = 512 * (4 * half + b)
+            n_t.append(done("t", ten.matmul_mx(T.ps[:, c:c + H], T.ec[:, 128 * b:128 * b + 128], T.es[:, 128 * b:128 * b + 128],
+                                               T.rc[:, a:a + H], T.rs[:, a:a + H], k == 0, k == N - 1)))
+        return n_t
+
+    def make_v(half, n_t):
+        vt = T["vt%d" % half]
+        for b in range(4):
+            c = 512 * (4 * half + b)
+            o, i = vt[:, b:4 * H:4], T.ps[:, c:c + H]
+            if b % 2 == 0:
+                need(sca, "s", "t", n_t[b])
+                n_s = done("s", sca.activation(o, i, COPY))
+            else:
+                need(vec, "v", "t", n_t[b])
+                n_v = done("v", vec.tensor_copy(o, i))
+        need(vec, "v", "v", n_v)
+        need(vec, "v", "s", n_s)
+        return done("v", vec.quantize_mx(T.vc[:, H * half:H * half + H], T.vs[:, H * half:H * half + H], vt[:, 0:4 * H]))
+
+    def times_w(half, n_q):
+        need(ten, "t", "v", n_w)
+        need(ten, "t", "v", n_q)
+        n = []
+        for o in range(O):
+            c = 512 * (2 * half + o)
+            n.append(done("t", ten.matmul_mx(T.ps[:, c:c + H], T.wc[:, 128 * o:128 * o + 128], T.wp[:, 128 * o:128 * o + 128],
+                                             T.vc[:, H * half:H * half + H], T.vs[:, H * half:H * half + H], True, True)))
+        return n
+
+    def store(half, n_y):
+        y0, y1 = H * half, TOK + H * half
+        c = 1024 * half
+        need(sca, "s", "t", n_y[0])
+        n_s = done("s", sca.activation(T.yo[:, y0:y0 + H], T.ps[:, c:c + H], COPY))
+        need(vec, "v", "t", n_y[1])
+        n_v = done("v", vec.tensor_copy(T.yo[:, y1:y1 + H], T.ps[:, c + 512:c + 512 + H]))
+        if half:
+            need(sca, "s", "s", n_s)
+            sca.dma_start(T.y[:, y0:y0 + H], T.yo[:, y0:y0 + H]).then_inc(T.sem.yd, 16)
+        else:
+            need(syn, "y", "s", n_s)
+            syn.dma_start(T.y[:, y0:y0 + H], T.yo[:, y0:y0 + H]).then_inc(T.sem.yd, 16)
+        need(syn, "y", "v", n_v)
+        syn.dma_start(T.y[:, y1:y1 + H], T.yo[:, y1:y1 + H]).then_inc(T.sem.yd, 16)
+
+    for k, q in enumerate(chain(r, 0, T, topo)):
+        n_a = add(0, k, q)
+    n_q = make_v(0, n_a)
+    for k, q in enumerate(chain(r, 1, T, topo)):
+        n_b = add(1, k, q)
+        if k == 2:
+            n_y = times_w(0, n_q)
+    store(0, n_y)
+    store(1, times_w(1, make_v(1, n_b)))
+    syn.wait_ge(T.sem.yd, 64)
+    g.wait_ge(T.sem.sent, state["sent"])

@@ -5,10 +5,22 @@ N, TOK, K, O = 8, 256, 256, 2
 H = TOK // 2
 HA = (1237, 1811, 947, 1543, 2017, 733, 1409, 1699)
 HB = (40503, 12289, 58111, 3571, 27644, 61007, 19211, 50021)
-SHARE = (2, 3, 2, 3, 2, 3, 2)
+UNITS = (
+    ((("f", 0, 0), ("p", 0, 0)), 3),
+    ((("f", 1, 0), ("p", 1, 0)), 2),
+    ((("f", 2, 0), ("p", 2, 0)), 3),
+    ((("m", 0, 0), ("f", 0, 1)), 2),
+    ((("f", 1, 1), ("f", 2, 1)), 2),
+    ((("p", 0, 1),), 3),
+    ((("p", 1, 1),), 2),
+    ((("p", 2, 1),), 3),
+    ((("m", 0, 1),), 2),
+)
+GROUPS = ((0, 2), (2, N - 1), (N - 1, 2 * (N - 1)))
+NEAR = 1
 SLOTS = 2 * (N - 1)
 LH = H // 16
-WIN = 4 * K - 3
+PLACES = 4
 
 SCRATCH = {
     "ids8": ("sbuf", [128, 16], "int32"),
@@ -19,8 +31,10 @@ SCRATCH = {
     "lx": ("sbuf", [128, LH * SLOTS], "int32"),
     "ly": ("sbuf", [128, LH * SLOTS], "int32"),
     "lo": ("sbuf", [128, LH * SLOTS], "uint16"),
+    "tbl": ("sbuf", [128, 4 * K], "bfloat16"),
     "ws": ("sbuf", [128, 512 * O], "bfloat16"),
-    "ones": ("sbuf", [128, 520], "bfloat16"),
+    "ones": ("sbuf", [128, 128], "bfloat16"),
+    "eye": ("sbuf", [128, 128], "bfloat16"),
     "ez": ("sbuf", [128, 520], "bfloat16"),
     "ec": ("sbuf", [128, 512], "float8_e4m3fn_x4"),
     "es": ("sbuf", [128, 512], "uint8"),
@@ -28,8 +42,9 @@ SCRATCH = {
     "wp": ("sbuf", [128, 128 * O], "uint8"),
     "rc": ("sbuf", [128, N * TOK], "float8_e4m3fn_x4"),
     "rs": ("sbuf", [128, N * TOK], "uint8"),
-    "hc": ("sbuf", [128, 4 * TOK], "float8_e4m3fn_x4"),
-    "hs": ("sbuf", [128, 4 * TOK], "uint8"),
+    "hc": ("sbuf", [128, PLACES * H], "float8_e4m3fn_x4"),
+    "hs": ("sbuf", [128, PLACES * H], "uint8"),
+    "ho": ("sbuf", [128, 4 * TOK], "bfloat16"),
     "vt0": ("sbuf", [128, 4 * H], "bfloat16"),
     "vt1": ("sbuf", [128, 4 * H], "bfloat16"),
     "vc": ("sbuf", [128, TOK], "float8_e4m3fn_x4"),
@@ -38,15 +53,14 @@ SCRATCH = {
     "ps": ("psum", [128, 512 * 8], "float32"),
 }
 for _i in range(4):
-    SCRATCH["tb%d" % _i] = ("sbuf", [128, 4 * K], "bfloat16")
-for _i in range(N):
-    SCRATCH["h%d" % _i] = ("sbuf", [128, 4 * TOK], "bfloat16")
-for _i in range(N - 1):
-    SCRATCH["qc%d" % _i] = ("sbuf", [128, TOK], "float8_e4m3fn_x4")
-    SCRATCH["qs%d" % _i] = ("sbuf", [128, TOK], "uint8")
+    SCRATCH["tp%d" % _i] = ("sbuf", [128, K], "bfloat16")
+for _i, (_u, _s) in enumerate(UNITS):
+    SCRATCH["h%d" % _i] = ("sbuf", [128, 4 * H * len(_u)], "bfloat16")
+    SCRATCH["qc%d" % _i] = ("sbuf", [128, H * len(_u)], "float8_e4m3fn_x4")
+    SCRATCH["qs%d" % _i] = ("sbuf", [128, H * len(_u)], "uint8")
 
 SEMAPHORES = ["idl", "tbl", "wl", "v", "s", "t", "ga", "lists0", "lists1", "lists2", "sent", "yd"]
-SEMAPHORES += ["hcode%d" % i for i in range(8)] + ["hplane%d" % i for i in range(8)]
+SEMAPHORES += ["hcode%d" % i for i in range(PLACES)] + ["hplane%d" % i for i in range(PLACES)]
 SEMAPHORES += ["arr%d_%d" % (h, q) for h in range(2) for q in range(N)]
 
 
@@ -62,43 +76,42 @@ def plan(core, T, topo):
     ch = topo.chip(core)
     r = T.rank_of(core)
     ring = [(r + k) % N for k in range(1, N)]
-    mate = [d for d in ring if topo.mates(ch, topo.chip(T.cores[d]))]
-    plane = [d for d in ring if topo.same_plane(ch, topo.chip(T.cores[d]))]
-    far = [d for d in ring if d not in mate and d not in plane]
+    kinds = {"m": [d for d in ring if topo.mates(ch, topo.chip(T.cores[d]))],
+             "p": [d for d in ring if topo.same_plane(ch, topo.chip(T.cores[d]))]}
+    kinds["f"] = far = [d for d in ring if d not in kinds["m"] and d not in kinds["p"]]
     help_ = [c for c in topo.cores_of(core)
              if topo.die(c) != topo.die(core) and all(topo.may_write(c, T.cores[d]) for d in far)]
     off = {e for d in ring for e in topo.engines(core, T.cores[d])}
     helper = {d: help_[i % len(help_)] for i, d in enumerate(far)}
-    D = plane + mate
-    first = far[:2] + D + far[2:]
-    second = far[2:] + far[:2] + D
-    slot = {(d, 0): i for i, d in enumerate(first)}
-    slot.update({(d, 1): N - 1 + i for i, d in enumerate(second)})
-    shape = [[(far[0], 0), (far[1], 0)], [(D[0], 0), (D[1], 0)], [(far[2], None)], [(D[2], 0), (D[3], 0)],
-             [(far[0], 1), (far[1], 1)], [(D[0], 1), (D[1], 1)], [(D[2], 1), (D[3], 1)]]
-    used = {c: [0, 0] for c in help_}
-    units = []
-    for u in shape:
+    near = [c for c in topo.cores_of(core) if topo.die(c) == topo.die(core) and c != core]
+    for i in range(NEAR):
+        helper[kinds["p"][i]] = near[i]
+    used = {c: 0 for c in help_ + near}
+    units, slot, turn = [], {}, 0
+    for u, _ in UNITS:
         pieces = []
-        for i, (d, half) in enumerate(u):
-            n = TOK if half is None else H
+        turn += H * len(u)
+        for i, (kind, k, half) in enumerate(u):
+            d = kinds[kind][k]
             via = helper.get(d)
-            if via is None:
-                e = topo.engines(core, T.cores[d])
-            else:
-                e = [x for x in topo.engines(core, via) if x not in off]
-            w = len(e) // len(u)
-            p = {"to": d, "half": half, "slot": slot[(d, half or 0)], "col": i * H, "n": n, "via": via, "mask": as_mask(e[i * w:i * w + w])}
+            slot[(d, half)] = len(slot)
+            p = {"to": d, "half": half, "slot": slot[(d, half)], "col": i * H, "via": via, "turn": turn}
             if via is not None:
-                p["place"], p["at"] = used[via]
-                used[via] = [p["place"] + 1, p["at"] + n]
+                p["place"] = used[via]
+                used[via] += 1
             pieces.append(p)
+        for direct in (True, False):
+            same = [p for p in pieces if (p["via"] is None or p["via"] in near and len(u) > 1) == direct]
+            for i, p in enumerate(same):
+                e = topo.engines(core, T.cores[p["to"]]) if direct else [x for x in topo.engines(core, p["via"]) if x not in off]
+                w = len(e) // len(same)
+                p["mask"] = as_mask(e[i * w:i * w + w])
         units.append(pieces)
     return units, slot
 
 
 def column(q, half):
-    return TOK * q + H * (half or 0)
+    return TOK * q + H * half
 
 
 def rank_program(g, core, T, topo):
@@ -120,26 +133,26 @@ def helper_program(g, core, T, topo):
             rid, pid, _ = topo.addr(dst)
             n_in = bits(p["mask"])
             m = topo.mask(core, dst)
-            arr = T.sem["arr%d_%d" % (p["half"] or 0, q)]
-            a, b, n = column(q, p["half"]), p["at"], p["n"]
+            arr = T.sem["arr%d_%d" % (p["half"], q)]
+            a, b = column(q, p["half"]), H * p["place"]
             g.wait_ge(T.sem["hcode%d" % p["place"]], n_in)
-            g.remote_dma(T.rc[:, a:a + n].bitcast(dt.uint8), T.hc[:, b:b + n].bitcast(dt.uint8), arr, T.sem.sent, pid, rid, m)
+            g.remote_dma(T.rc[:, a:a + H].bitcast(dt.uint8), T.hc[:, b:b + H].bitcast(dt.uint8), arr, T.sem.sent, pid, rid, m)
             g.wait_ge(T.sem["hplane%d" % p["place"]], n_in)
-            g.remote_dma(T.rs[:, a:a + n], T.hs[:, b:b + n], arr, T.sem.sent, pid, rid, m)
+            g.remote_dma(T.rs[:, a:a + H], T.hs[:, b:b + H], arr, T.sem.sent, pid, rid, m)
             total += 2 * bits(m)
     if total:
         g.wait_ge(T.sem.sent, total)
 
 
 def arrival(q, r, half, T, topo):
-    for i, u in enumerate(plan(T.cores[q], T, topo)[0]):
+    for u in plan(T.cores[q], T, topo)[0]:
         for p in u:
-            if p["to"] == r and p["half"] in (half, None):
+            if p["to"] == r and p["half"] == half:
                 if p["via"] is None:
-                    m, hops = p["mask"], 2
+                    m, hops = p["mask"], 1
                 else:
-                    m, hops = topo.mask(p["via"], T.cores[r]), 4
-                return i + hops, "arr%d_%d" % (p["half"] or 0, q), 2 * bits(m)
+                    m, hops = topo.mask(p["via"], T.cores[r]), 2
+                return p["turn"] + 2 * TOK * hops, "arr%d_%d" % (half, q), 2 * bits(m)
 
 
 def chain(r, half, T, topo):
@@ -168,13 +181,13 @@ def owner_program(g, core, r, T, topo):
 
     for i in range(8):
         (syn if i < 4 else sca).dma_start(T.ids8[16 * i:16 * i + 16, :], T.ids[:, :]).then_inc(T.sem.idl, 16)
-    syn.dma_start(T.tb0[:, :], T.tb[:, :]).then_inc(T.sem.tbl, 16)
+    syn.dma_start(T.tbl[:, :], T.tb[:, :]).then_inc(T.sem.tbl, 16)
 
     n_ones = done("v", vec.memset(T.ones[:, :], 1.0))
+    n_z = done("v", vec.memset(T.ez[:, :], 0.0))
     g.wait_ge(T.sem.v, n_ones)
-    g.affine_select(T.ez[:, :], T.ones[:, :], [[1, 520]], A.is_equal, 0.0, -4, -4).then_inc(T.sem.ga, 1)
+    g.affine_select(T.eye[:, :], T.ones[:, :], [[-1, 128]], A.is_equal, 0.0, 0, 1).then_inc(T.sem.ga, 1)
 
-    GROUPS = ((0, 4), (4, N - 1), (N - 1, SLOTS))
     g.wait_ge(T.sem.idl, 128)
     sent = 0
     mine = {d: plan(T.cores[d], T, topo)[1] for d in others}
@@ -196,110 +209,118 @@ def owner_program(g, core, r, T, topo):
     state = {"sent": sent}
 
     vec.wait_ge(T.sem.ga, 1)
+    need(vec, "v", "v", n_z)
+    need(vec, "v", "v", done("v", vec.tensor_copy(T.ez[:, 4:516:4], T.eye[:, :])))
     for b in range(4):
         n_e = done("v", vec.quantize_mx(T.ec[:, 128 * b:128 * b + 128], T.es[:, 128 * b:128 * b + 128], T.ez[:, 4 - b:4 - b + 512]))
 
-    def hashes(src, x, y, off, a, b):
-        n = done("v", vec.tensor_scalar(x[:, a:b], src[:, a:b], HA[r], HB[r], A.mult, A.add))
-        need(vec, "v", "v", n)
-        n = done("v", vec.tensor_scalar(y[:, a:b], x[:, a:b], 3, 4 * (K - 1), A.arith_shift_right, A.bitwise_and))
-        need(vec, "v", "v", n)
-        return done("v", vec.tensor_copy(off[:, a:b], y[:, a:b]))
+    def hash_steps(src, x, y, off, a, b):
+        return [lambda: vec.tensor_scalar(x[:, a:b], src[:, a:b], HA[r], HB[r], A.mult, A.add),
+                lambda: vec.tensor_scalar(y[:, a:b], x[:, a:b], 5, K - 1, A.arith_shift_right, A.bitwise_and),
+                lambda: vec.tensor_copy(off[:, a:b], y[:, a:b])]
 
-    def pick(eng, me, h, off, t, n_off):
+    def run(steps, n=0):
+        for step in steps:
+            need(vec, "v", "v", n)
+            n = done("v", step())
+        return n
+
+    def pick(eng, me, h, n, off, t, n_off):
         need(eng, me, "v", n_off)
-        if t:
-            need(eng, me, moved[t][0], moved[t][1])
-        o, i = h[:, t:4 * TOK:4], T["tb%d" % t][:, 0:WIN].indirect(off)
+        need(eng, me, planes_[t][0], planes_[t][1])
+        o, i = h[:, t:4 * n:4], T["tp%d" % t][:, 0:K].indirect(off)
         return done(me, sca.activation(o, i, COPY) if me == "s" else vec.tensor_copy(o, i))
-
-    vec.wait_ge(T.sem.idl, 128)
-    n_oo = hashes(T.ids8, T.ox, T.oy, T.oo, 0, 16)
-    own = {"h": T["h%d" % (N - 1)], "c": T.rc[:, TOK * r:TOK * r + TOK], "p": T.rs[:, TOK * r:TOK * r + TOK]}
-    moved = {}
-    sca.wait_ge(T.sem.tbl, 16)
-    moved[1] = ("s", done("s", sca.activation(T.tb1[:, 0:WIN], T.tb0[:, 1:1 + WIN], COPY)))
-    vec.wait_ge(T.sem.tbl, 16)
-    for t in (2, 3):
-        moved[t] = ("v", done("v", vec.tensor_copy(T["tb%d" % t][:, 0:WIN], T.tb0[:, t:t + WIN])))
-    for t in (0, 1):
-        own["s"] = pick(sca, "s", own["h"], T.oo[:, 0:16], t, n_oo)
-    for t in (2, 3):
-        own["v"] = pick(vec, "v", own["h"], T.oo[:, 0:16], t, n_oo)
 
     def pack(u):
         need(vec, "v", "v", u["v"])
         need(vec, "v", "s", u["s"])
-        return done("v", vec.quantize_mx(u["c"], u["p"], u["h"][:, 0:4 * TOK]))
+        return done("v", vec.quantize_mx(u["c"], u["p"], u["h"][:, 0:4 * u["n"]]))
+
+    vec.wait_ge(T.sem.idl, 128)
+    n_oo = run(hash_steps(T.ids8, T.ox, T.oy, T.oo, 0, 16))
+    own = {"h": T.ho, "n": TOK, "c": T.rc[:, TOK * r:TOK * r + TOK], "p": T.rs[:, TOK * r:TOK * r + TOK]}
+    planes_ = {}
+    sca.wait_ge(T.sem.tbl, 16)
+    planes_[0] = ("s", done("s", sca.activation(T.tp0[:, :], T.tbl[:, 0:4 * K:4], COPY)))
+    vec.wait_ge(T.sem.tbl, 16)
+    for t in (1, 2, 3):
+        planes_[t] = ("v", done("v", vec.tensor_copy(T["tp%d" % t][:, :], T.tbl[:, t:4 * K:4])))
+    for t in (0, 1):
+        own["s"] = pick(sca, "s", own["h"], TOK, T.oo[:, 0:16], t, n_oo)
+    for t in (2, 3):
+        own["v"] = pick(vec, "v", own["h"], TOK, T.oo[:, 0:16], t, n_oo)
+    n_own = pack(own)
 
     def pack_and_send(u):
-        n = pack(u)
-        if "pieces" not in u:
-            u["n"] = n
-            return
-        g.wait_ge(T.sem.v, n)
+        g.wait_ge(T.sem.v, pack(u))
         codes, planes = [], []
         for p in u["pieces"]:
-            a, c, w = column(r, p["half"]), p["col"], p["n"]
+            a, c = column(r, p["half"]), p["col"]
             if p["via"] is None:
-                dst, oc, op = T.cores[p["to"]], T.rc[:, a:a + w], T.rs[:, a:a + w]
-                sc = sp = T.sem["arr%d_%d" % (p["half"] or 0, r)]
+                dst, oc, op = T.cores[p["to"]], T.rc[:, a:a + H], T.rs[:, a:a + H]
+                sc = sp = T.sem["arr%d_%d" % (p["half"], r)]
             else:
-                b = p["at"]
-                dst, oc, op = p["via"], T.hc[:, b:b + w], T.hs[:, b:b + w]
+                b = H * p["place"]
+                dst, oc, op = p["via"], T.hc[:, b:b + H], T.hs[:, b:b + H]
                 sc, sp = T.sem["hcode%d" % p["place"]], T.sem["hplane%d" % p["place"]]
             rid, pid, _ = topo.addr(dst)
             to = [DstId(rid=rid, pnc=pid)]
-            codes.append(RemoteDMATransfer(dst_ids=to, dma_engine_mask=p["mask"], remote_sem=sc, srcs=[u["c"][c:c + w].bitcast(dt.uint8)] if False else [u["qc"][:, c:c + w].bitcast(dt.uint8)], dsts=[oc.bitcast(dt.uint8)]))
-            planes.append(RemoteDMATransfer(dst_ids=to, dma_engine_mask=p["mask"], remote_sem=sp, srcs=[u["qs"][:, c:c + w]], dsts=[op]))
+            codes.append(RemoteDMATransfer(dst_ids=to, dma_engine_mask=p["mask"], remote_sem=sc, srcs=[u["qc"][:, c:c + H].bitcast(dt.uint8)], dsts=[oc.bitcast(dt.uint8)]))
+            planes.append(RemoteDMATransfer(dst_ids=to, dma_engine_mask=p["mask"], remote_sem=sp, srcs=[u["qs"][:, c:c + H]], dsts=[op]))
             state["sent"] += 2 * bits(p["mask"])
         g.remote_dma_fused(codes, local_sem=T.sem.sent)
         g.remote_dma_fused(planes, local_sem=T.sem.sent)
 
     n_of = {}
 
-    def listed(ks):
-        for k in ks:
-            vec.wait_ge(T.sem["lists%d" % k], each * (GROUPS[k][1] - GROUPS[k][0]))
-        a, b = GROUPS[ks[0]][0], GROUPS[ks[-1]][1]
-        n = hashes(T.lst, T.lx, T.ly, T.lo, LH * a, LH * b)
-        for i in range(a, b):
+    def listed(k):
+        a, b = GROUPS[k]
+        vec.wait_ge(T.sem["lists%d" % k], each * (b - a))
+        return hash_steps(T.lst, T.lx, T.ly, T.lo, LH * a, LH * b)
+
+    def known(k, n):
+        for i in range(*GROUPS[k]):
             n_of[i] = n
 
-    listed([0])
-    before = own
+    known(0, run(listed(0)))
+    before = None
     for i, pieces in enumerate(units):
-        u = {"h": T["h%d" % i], "qc": T["qc%d" % i], "qs": T["qs%d" % i], "c": T["qc%d" % i][:, 0:TOK], "p": T["qs%d" % i][:, 0:TOK], "pieces": pieces}
+        n = H * len(pieces)
+        u = {"h": T["h%d" % i], "n": n, "qc": T["qc%d" % i], "qs": T["qs%d" % i], "c": T["qc%d" % i][:, 0:n], "p": T["qs%d" % i][:, 0:n], "pieces": pieces}
         s = pieces[0]["slot"]
-        off = T.lo[:, LH * s:LH * s + 2 * LH]
-        for t in range(SHARE[i]):
-            u["s"] = pick(sca, "s", u["h"], off, t, n_of[s + 1])
-        for t in range(SHARE[i], 4):
-            u["v"] = pick(vec, "v", u["h"], off, t, n_of[s + 1])
+        off = T.lo[:, LH * s:LH * (s + len(pieces))]
+        n_off = n_of[s + len(pieces) - 1]
+        share = UNITS[i][1]
+        steps = listed(2) if i == 1 else []
+        n_h = run(steps[:1])
+        for t in range(share):
+            u["s"] = pick(sca, "s", u["h"], n, off, t, n_off)
+        for t in range(share, 4):
+            u["v"] = pick(vec, "v", u["h"], n, off, t, n_off)
+            n_h = run(steps[1 + t - share:2 + t - share], n_h)
             if before is not None:
                 pack_and_send(before)
                 before = None
         before = u
+        if i == 0:
+            known(1, run(listed(1)))
         if i == 1:
-            listed([1, 2])
+            known(2, n_h)
     pack_and_send(before)
 
-    syn.wait_ge(T.sem.lists0, each * GROUPS[0][1])
+    syn.wait_ge(T.sem.lists2, each * (GROUPS[2][1] - GROUPS[2][0]))
     syn.dma_start(T.ws[:, :], T.w[:, :]).then_inc(T.sem.wl, 16)
     vec.wait_ge(T.sem.wl, 16)
     n_w = done("v", vec.quantize_mx(T.wc[:, 0:128 * O], T.wp[:, 0:128 * O], T.ws[:, 0:512 * O]))
 
     need(ten, "t", "v", n_e)
-    waited = {}
 
     def add(half, k, q):
         if q == r:
-            need(ten, "t", "v", own["n"])
+            need(ten, "t", "v", n_own)
         else:
             _, sem, n = arrival(q, r, half, T, topo)
-            if sem not in waited:
-                ten.wait_ge(T.sem[sem], n)
-                waited[sem] = n
+            ten.wait_ge(T.sem[sem], n)
         a, n_t = column(q, half), []
         for b in range(4):
             c = 512 * (4 * half + b)
@@ -332,30 +353,26 @@ def owner_program(g, core, r, T, topo):
                                              T.vc[:, H * half:H * half + H], T.vs[:, H * half:H * half + H], True, True)))
         return n
 
-    def store(half, n_y):
-        y0, y1 = H * half, TOK + H * half
-        c = 1024 * half
-        need(sca, "s", "t", n_y[0])
-        n_s = done("s", sca.activation(T.yo[:, y0:y0 + H], T.ps[:, c:c + H], COPY))
-        need(vec, "v", "t", n_y[1])
-        n_v = done("v", vec.tensor_copy(T.yo[:, y1:y1 + H], T.ps[:, c + 512:c + 512 + H]))
-        if half:
-            need(sca, "s", "s", n_s)
-            sca.dma_start(T.y[:, y0:y0 + H], T.yo[:, y0:y0 + H]).then_inc(T.sem.yd, 16)
-        else:
-            need(syn, "y", "s", n_s)
-            syn.dma_start(T.y[:, y0:y0 + H], T.yo[:, y0:y0 + H]).then_inc(T.sem.yd, 16)
-        need(syn, "y", "v", n_v)
-        syn.dma_start(T.y[:, y1:y1 + H], T.yo[:, y1:y1 + H]).then_inc(T.sem.yd, 16)
+    def store(half, o, me, n_y, queue, name):
+        y0, c = TOK * o + H * half, 512 * (2 * half + o)
+        eng = sca if me == "s" else vec
+        need(eng, me, "t", n_y[o])
+        out, in_ = T.yo[:, y0:y0 + H], T.ps[:, c:c + H]
+        n = done(me, sca.activation(out, in_, COPY) if me == "s" else vec.tensor_copy(out, in_))
+        need(queue, name, me, n)
+        queue.dma_start(T.y[:, y0:y0 + H], T.yo[:, y0:y0 + H]).then_inc(T.sem.yd, 16)
 
     for k, q in enumerate(chain(r, 0, T, topo)):
         n_a = add(0, k, q)
-    n_q = make_v(0, n_a)
+    n_q0 = make_v(0, n_a)
     for k, q in enumerate(chain(r, 1, T, topo)):
         n_b = add(1, k, q)
-        if k == 2:
-            n_y = times_w(0, n_q)
-    store(0, n_y)
-    store(1, times_w(1, make_v(1, n_b)))
+    n_y0 = times_w(0, n_q0)
+    n_q1 = make_v(1, n_b)
+    for o in range(O):
+        store(0, o, "s", n_y0, syn, "y")
+    n_y1 = times_w(1, n_q1)
+    store(1, 0, "s", n_y1, sca, "s")
+    store(1, 1, "v", n_y1, syn, "y")
     syn.wait_ge(T.sem.yd, 64)
     g.wait_ge(T.sem.sent, state["sent"])

@@ -6,30 +6,32 @@ H = TOK // 2
 HA = (1237, 1811, 947, 1543, 2017, 733, 1409, 1699)
 HB = (40503, 12289, 58111, 3571, 27644, 61007, 19211, 50021)
 UNITS = (
-    ((("f", 0, 0), ("p", 0, 0)), 3),
-    ((("f", 1, 0), ("p", 1, 0)), 2),
-    ((("f", 2, 0), ("p", 2, 0)), 3),
-    ((("m", 0, 0), ("f", 0, 1)), 2),
-    ((("f", 1, 1), ("f", 2, 1)), 2),
-    ((("p", 0, 1),), 3),
-    ((("p", 1, 1),), 2),
-    ((("p", 2, 1),), 3),
-    ((("m", 0, 1),), 2),
+    ((("p0", 0, "n0"), ("f0", 0, "x0")), 2),
+    ((("p1", 0, ""), ("f1", 0, "x1")), 3),
+    ((("f2", 0, "x0"), ("p2", 0, "")), 2),
+    ((("f0", 1, "x0"), ("m0", 0, "")), 2),
+    ((("f1", 1, "x1"), ("f2", 1, "x0")), 2),
+    ((("p0", 1, "n0"),), 3),
+    ((("p1", 1, ""),), 2),
+    ((("p2", 1, ""),), 3),
+    ((("m0", 1, ""),), 2),
 )
-GROUPS = ((0, 2), (2, N - 1), (N - 1, 2 * (N - 1)))
-NEAR = 1
+LAYOUT = (("m0", 0), ("m0", 1), ("p1", 1), ("p1", 0), ("f1", 0), ("f1", 1), ("f2", 1), ("f2", 0), ("p2", 0), ("p2", 1))
+LAYOUT = (("p0", 1), ("p0", 0), ("f0", 0), ("f0", 1)) + LAYOUT
+RAW = "m0"
+LISTS = (2, 2, 2)
 SLOTS = 2 * (N - 1)
 LH = H // 16
 PLACES = 4
 
 SCRATCH = {
     "ids8": ("sbuf", [128, 16], "int32"),
-    "ox": ("sbuf", [128, 16], "int32"),
-    "oy": ("sbuf", [128, 16], "int32"),
-    "oo": ("sbuf", [128, 16], "uint16"),
-    "lst": ("sbuf", [128, LH * SLOTS], "int32"),
-    "lx": ("sbuf", [128, LH * SLOTS], "int32"),
-    "ly": ("sbuf", [128, LH * SLOTS], "int32"),
+    "ox": ("sbuf", [128, N - 1, 2 * LH], "int32"),
+    "oy": ("sbuf", [128, N - 1, 2 * LH], "int32"),
+    "oo": ("sbuf", [128, N - 1, 2 * LH], "uint16"),
+    "lst": ("sbuf", [128, 2 * LH], "int32"),
+    "lx": ("sbuf", [128, 2 * LH], "int32"),
+    "ly": ("sbuf", [128, 2 * LH], "int32"),
     "lo": ("sbuf", [128, LH * SLOTS], "uint16"),
     "tbl": ("sbuf", [128, 4 * K], "bfloat16"),
     "ws": ("sbuf", [128, 512 * O], "bfloat16"),
@@ -44,9 +46,9 @@ SCRATCH = {
     "rs": ("sbuf", [128, N * TOK], "uint8"),
     "hc": ("sbuf", [128, PLACES * H], "float8_e4m3fn_x4"),
     "hs": ("sbuf", [128, PLACES * H], "uint8"),
-    "ho": ("sbuf", [128, 4 * TOK], "bfloat16"),
-    "vt0": ("sbuf", [128, 4 * H], "bfloat16"),
-    "vt1": ("sbuf", [128, 4 * H], "bfloat16"),
+    "ho0": ("sbuf", [128, 4 * H], "bfloat16"),
+    "ho1": ("sbuf", [128, 4 * H], "bfloat16"),
+    "vt": ("sbuf", [128, 4 * H], "bfloat16"),
     "vc": ("sbuf", [128, TOK], "float8_e4m3fn_x4"),
     "vs": ("sbuf", [128, TOK], "uint8"),
     "yo": ("sbuf", [128, O * TOK], "float32"),
@@ -59,7 +61,8 @@ for _i, (_u, _s) in enumerate(UNITS):
     SCRATCH["qc%d" % _i] = ("sbuf", [128, H * len(_u)], "float8_e4m3fn_x4")
     SCRATCH["qs%d" % _i] = ("sbuf", [128, H * len(_u)], "uint8")
 
-SEMAPHORES = ["idl", "tbl", "wl", "v", "s", "t", "ga", "lists0", "lists1", "lists2", "sent", "yd"]
+SEMAPHORES = ["idl", "tbl", "wl", "v", "s", "t", "ga", "v0", "raw", "sent", "yd"]
+SEMAPHORES += ["lists%d" % i for i in range(len(LISTS))]
 SEMAPHORES += ["hcode%d" % i for i in range(PLACES)] + ["hplane%d" % i for i in range(PLACES)]
 SEMAPHORES += ["arr%d_%d" % (h, q) for h in range(2) for q in range(N)]
 
@@ -76,72 +79,78 @@ def plan(core, T, topo):
     ch = topo.chip(core)
     r = T.rank_of(core)
     ring = [(r + k) % N for k in range(1, N)]
-    kinds = {"m": [d for d in ring if topo.mates(ch, topo.chip(T.cores[d]))],
-             "p": [d for d in ring if topo.same_plane(ch, topo.chip(T.cores[d]))]}
-    kinds["f"] = far = [d for d in ring if d not in kinds["m"] and d not in kinds["p"]]
-    help_ = [c for c in topo.cores_of(core)
-             if topo.die(c) != topo.die(core) and all(topo.may_write(c, T.cores[d]) for d in far)]
-    off = {e for d in ring for e in topo.engines(core, T.cores[d])}
-    helper = {d: help_[i % len(help_)] for i, d in enumerate(far)}
-    near = [c for c in topo.cores_of(core) if topo.die(c) == topo.die(core) and c != core]
-    for i in range(NEAR):
-        helper[kinds["p"][i]] = near[i]
-    used = {c: 0 for c in help_ + near}
+    who = {"m": [d for d in ring if topo.mates(ch, topo.chip(T.cores[d]))],
+           "p": [d for d in ring if topo.same_plane(ch, topo.chip(T.cores[d]))]}
+    who["f"] = [d for d in ring if d not in who["m"] and d not in who["p"]]
+    who["x"] = [c for c in topo.cores_of(core)
+                if topo.die(c) != topo.die(core) and all(topo.may_write(c, T.cores[d]) for d in who["f"])]
+    who["n"] = [c for c in topo.cores_of(core) if topo.die(c) == topo.die(core) and c != core]
+    off = sorted({e for d in ring for e in topo.engines(core, T.cores[d])})
+    every = topo.engines(core, who["n"][0])
+    inner = [e for e in every if e not in off]
+    used = {}
     units, slot, turn = [], {}, 0
     for u, _ in UNITS:
         pieces = []
         turn += H * len(u)
-        for i, (kind, k, half) in enumerate(u):
-            d = kinds[kind][k]
-            via = helper.get(d)
-            slot[(d, half)] = len(slot)
-            p = {"to": d, "half": half, "slot": slot[(d, half)], "col": i * H, "via": via, "turn": turn}
+        for i, (to, half, way) in enumerate(u):
+            d = who[to[0]][int(to[1])]
+            via = who[way[0]][int(way[1])] if way else None
+            slot[(d, half)] = LAYOUT.index((to, half))
+            p = {"to": d, "half": half, "slot": slot[(d, half)], "col": i * H, "cols": H, "via": via, "turn": turn}
             if via is not None:
-                p["place"] = used[via]
-                used[via] += 1
+                p["place"] = p["head"] = used.get(via, 0)
+                used[via] = p["place"] + 1
             pieces.append(p)
-        for direct in (True, False):
-            same = [p for p in pieces if (p["via"] is None or p["via"] in near and len(u) > 1) == direct]
-            for i, p in enumerate(same):
-                e = topo.engines(core, T.cores[p["to"]]) if direct else [x for x in topo.engines(core, p["via"]) if x not in off]
-                w = len(e) // len(same)
-                p["mask"] = as_mask(e[i * w:i * w + w])
+        relayed = [p for p in pieces if p["via"] is not None]
+        direct = [p for p in pieces if p["via"] is None]
+        if len(relayed) > 1 and len({p["via"] for p in pieces}) == 1:
+            for p in pieces:
+                p.update(mask=as_mask(every), head=pieces[0]["place"], cols=H * len(u) if p is pieces[0] else 0)
+        else:
+            rest = relayed[1:] + direct
+            for p in relayed[:1]:
+                p["mask"] = as_mask(inner)
+            for i, p in enumerate(rest):
+                w = len(off) // len(rest)
+                p["mask"] = as_mask(off[i * w:i * w + w])
         units.append(pieces)
     return units, slot
+
+
+def places(slot):
+    out = {}
+    for d, half in sorted(slot, key=slot.get):
+        out.setdefault(d, len(out))
+    return out
+
+
+def runs(slot, lo, hi):
+    at = places(slot)
+    todo = [(s, 2 * at[d] + half) for (d, half), s in sorted(slot.items(), key=lambda x: x[1]) if lo <= at[d] < hi]
+    out, i = [], 0
+    while i < len(todo):
+        s, a = todo[i]
+        step = max(todo[i + 1][1] - a, 1) if i + 1 < len(todo) else 1
+        n = 1
+        while i + n < len(todo) and todo[i + n] == (s + n, a + n * step):
+            n += 1
+        out.append((s, range(a, a + (n - 1) * step + 1, step)))
+        i += n
+    return out
 
 
 def column(q, half):
     return TOK * q + H * half
 
 
-def rank_program(g, core, T, topo):
-    rank = T.rank_of(core)
-    if rank is None:
-        helper_program(g, core, T, topo)
-        return
-    owner_program(g, core, rank, T, topo)
+def summer(r, half, T, topo):
+    core = T.cores[r]
+    return core if half else [c for c in topo.cores_of(core) if topo.die(c) == topo.die(core) and c != core][0]
 
 
-def helper_program(g, core, T, topo):
-    total = 0
-    for src in T.cores:
-        if topo.chip(src) != topo.chip(core):
-            continue
-        q = T.rank_of(src)
-        for p in [p for u in plan(src, T, topo)[0] for p in u if p["via"] == core]:
-            dst = T.cores[p["to"]]
-            rid, pid, _ = topo.addr(dst)
-            n_in = bits(p["mask"])
-            m = topo.mask(core, dst)
-            arr = T.sem["arr%d_%d" % (p["half"], q)]
-            a, b = column(q, p["half"]), H * p["place"]
-            g.wait_ge(T.sem["hcode%d" % p["place"]], n_in)
-            g.remote_dma(T.rc[:, a:a + H].bitcast(dt.uint8), T.hc[:, b:b + H].bitcast(dt.uint8), arr, T.sem.sent, pid, rid, m)
-            g.wait_ge(T.sem["hplane%d" % p["place"]], n_in)
-            g.remote_dma(T.rs[:, a:a + H], T.hs[:, b:b + H], arr, T.sem.sent, pid, rid, m)
-            total += 2 * bits(m)
-    if total:
-        g.wait_ge(T.sem.sent, total)
+def outside(src, T, topo):
+    return [topo.mask(src, c) for c in T.cores if topo.chip(c) != topo.chip(src) and topo.may_write(src, c)][0]
 
 
 def arrival(q, r, half, T, topo):
@@ -159,8 +168,23 @@ def chain(r, half, T, topo):
     return sorted([0, 1], key=lambda q: 0 if q == r else arrival(q, r, half, T, topo)[0]) + list(range(2, N))
 
 
-def owner_program(g, core, r, T, topo):
-    vec, sca, ten, syn = g.vector, g.scalar, g.tensor, g.sync
+def send_pair(g, T, topo, dst, mask, sem_c, sem_p, oc, ic, op, ip):
+    rid, pid, _ = topo.addr(dst)
+    g.remote_dma(oc.bitcast(dt.uint8), ic.bitcast(dt.uint8), sem_c, T.sem.sent, pid, rid, mask)
+    g.remote_dma(op, ip, sem_p, T.sem.sent, pid, rid, mask)
+    return 2 * bits(mask)
+
+
+def rank_program(g, core, T, topo):
+    rank = T.rank_of(core)
+    if rank is None:
+        helper_program(g, core, T, topo)
+        return
+    owner_program(g, core, rank, T, topo)
+
+
+def compute(g, T, topo):
+    vec, sca, ten = g.vector, g.scalar, g.tensor
     A = AluOpType
     COPY = ActivationFunctionType.Copy
     cnt = {"v": 0, "s": 0, "t": 0}
@@ -176,53 +200,126 @@ def owner_program(g, core, r, T, topo):
             queue.wait_ge(T.sem[name], val)
             seen[(me, name)] = val
 
-    units, _ = plan(core, T, topo)
+    def constants():
+        n_ones = done("v", vec.memset(T.ones[:, :], 1.0))
+        n_z = done("v", vec.memset(T.ez[:, :], 0.0))
+        g.wait_ge(T.sem.v, n_ones)
+        g.affine_select(T.eye[:, :], T.ones[:, :], [[-1, 128]], A.is_equal, 0.0, 0, 1).then_inc(T.sem.ga, 1)
+        vec.wait_ge(T.sem.ga, 1)
+        need(vec, "v", "v", n_z)
+        need(vec, "v", "v", done("v", vec.tensor_copy(T.ez[:, 4:516:4], T.eye[:, :])))
+        for b in range(4):
+            n_e = done("v", vec.quantize_mx(T.ec[:, 128 * b:128 * b + 128], T.es[:, 128 * b:128 * b + 128], T.ez[:, 4 - b:4 - b + 512]))
+        need(ten, "t", "v", n_e)
+
+    def add_up(r, half, own):
+        for k, q in enumerate(chain(r, half, T, topo)):
+            if q == r:
+                own()
+            else:
+                _, sem, n = arrival(q, r, half, T, topo)
+                ten.wait_ge(T.sem[sem], n)
+            a, n_t = column(q, half), []
+            for b in range(4):
+                n_t.append(done("t", ten.matmul_mx(T.ps[:, 512 * b:512 * b + H], T.ec[:, 128 * b:128 * b + 128], T.es[:, 128 * b:128 * b + 128],
+                                                   T.rc[:, a:a + H], T.rs[:, a:a + H], k == 0, k == N - 1)))
+        return n_t
+
+    def make_v(half, n_t):
+        for b in range(4):
+            o, i = T.vt[:, b:4 * H:4], T.ps[:, 512 * b:512 * b + H]
+            if b % 2 == 0:
+                need(sca, "s", "t", n_t[b])
+                n_s = done("s", sca.activation(o, i, COPY))
+            else:
+                need(vec, "v", "t", n_t[b])
+                n_v = done("v", vec.tensor_copy(o, i))
+        need(vec, "v", "v", n_v)
+        need(vec, "v", "s", n_s)
+        return done("v", vec.quantize_mx(T.vc[:, H * half:H * half + H], T.vs[:, H * half:H * half + H], T.vt[:, 0:4 * H]))
+
+    return done, need, constants, add_up, make_v
+
+
+def helper_program(g, core, T, topo):
+    src = [c for c in T.cores if topo.chip(c) == topo.chip(core)][0]
+    q = T.rank_of(src)
+    adds = summer(q, 0, T, topo) == core
+    if adds:
+        done, need, constants, add_up, make_v = compute(g, T, topo)
+        constants()
+        own = topo.mask(src, core) & ~outside(src, T, topo)
+        n_v = make_v(0, add_up(q, 0, lambda: g.tensor.wait_ge(T.sem["arr0_%d" % q], 2 * bits(own))))
+    total = 0
+    for p in [p for u in plan(src, T, topo)[0] for p in u if p["via"] == core]:
+        dst = summer(p["to"], p["half"], T, topo)
+        rid, pid, _ = topo.addr(dst)
+        m = topo.mask(core, dst)
+        arr = T.sem["arr%d_%d" % (p["half"], q)]
+        a, b = column(q, p["half"]), H * p["place"]
+        if p["cols"]:
+            g.wait_ge(T.sem["hcode%d" % p["head"]], bits(p["mask"]))
+        g.remote_dma(T.rc[:, a:a + H].bitcast(dt.uint8), T.hc[:, b:b + H].bitcast(dt.uint8), arr, T.sem.sent, pid, rid, m)
+        if p["cols"]:
+            g.wait_ge(T.sem["hplane%d" % p["head"]], bits(p["mask"]))
+        g.remote_dma(T.rs[:, a:a + H], T.hs[:, b:b + H], arr, T.sem.sent, pid, rid, m)
+        total += 2 * bits(m)
+    if adds:
+        g.wait_ge(T.sem.v, n_v)
+        total += send_pair(g, T, topo, src, topo.mask(core, src) & ~outside(core, T, topo), T.sem.v0, T.sem.v0, T.vc[:, 0:H], T.vc[:, 0:H], T.vs[:, 0:H], T.vs[:, 0:H])
+    if total:
+        g.wait_ge(T.sem.sent, total)
+
+
+def owner_program(g, core, r, T, topo):
+    vec, sca, ten, syn = g.vector, g.scalar, g.tensor, g.sync
+    A = AluOpType
+    COPY = ActivationFunctionType.Copy
+    done, need, constants, add_up, make_v = compute(g, T, topo)
+    units, slot = plan(core, T, topo)
     others = [d for d in range(N) if d != r]
+    groups = [(sum(LISTS[:k]), sum(LISTS[:k + 1])) for k in range(len(LISTS))]
 
     for i in range(8):
         (syn if i < 4 else sca).dma_start(T.ids8[16 * i:16 * i + 16, :], T.ids[:, :]).then_inc(T.sem.idl, 16)
     syn.dma_start(T.tbl[:, :], T.tb[:, :]).then_inc(T.sem.tbl, 16)
 
-    n_ones = done("v", vec.memset(T.ones[:, :], 1.0))
-    n_z = done("v", vec.memset(T.ez[:, :], 0.0))
-    g.wait_ge(T.sem.v, n_ones)
-    g.affine_select(T.eye[:, :], T.ones[:, :], [[-1, 128]], A.is_equal, 0.0, 0, 1).then_inc(T.sem.ga, 1)
+    constants()
 
     g.wait_ge(T.sem.idl, 128)
-    sent = 0
-    mine = {d: plan(T.cores[d], T, topo)[1] for d in others}
-    for k, (lo_, hi_) in enumerate(GROUPS):
-        ids_, dsts, mask, half = [], [], None, k // 2
-        for d in sorted(others, key=lambda x: mine[x][(r, half)]):
-            s = mine[d][(r, half)]
-            if not lo_ <= s < hi_:
-                continue
-            dst = T.cores[d]
-            rid, pid, _ = topo.addr(dst)
-            ids_.append(DstId(rid=rid, pnc=pid))
-            dsts.append(T.lst[:, LH * s:LH * s + LH])
-            m = topo.mask(core, dst)
-            mask = m if mask is None else mask & m
-        sent += bits(mask)
-        g.remote_dma_fused([RemoteDMATransfer(dst_ids=ids_, dma_engine_mask=mask, remote_sem=T.sem["lists%d" % k], srcs=[T.ids8[:, LH * half:LH * half + LH]], dsts=dsts)], local_sem=T.sem.sent)
+    mask = outside(core, T, topo)
     each = bits(mask)
-    state = {"sent": sent}
+    state = {"sent": 0}
+    mine = {d: [plan(T.cores[d], T, topo)[1][(r, half)] for half in range(2)] for d in others}
+    order = sorted(others, key=mine.get)
+    raw = [d for d in order if LAYOUT[mine[d][0]][0] == RAW][0]
+    order.remove(raw)
+    rid, pid, _ = topo.addr(T.cores[raw])
+    g.remote_dma(T.lst[:, :], T.ids8[:, :], T.sem.raw, T.sem.sent, pid, rid, mask)
+    state["sent"] += each
 
-    vec.wait_ge(T.sem.ga, 1)
-    need(vec, "v", "v", n_z)
-    need(vec, "v", "v", done("v", vec.tensor_copy(T.ez[:, 4:516:4], T.eye[:, :])))
-    for b in range(4):
-        n_e = done("v", vec.quantize_mx(T.ec[:, 128 * b:128 * b + 128], T.es[:, 128 * b:128 * b + 128], T.ez[:, 4 - b:4 - b + 512]))
+    def hashes(srcs, x, y, off):
+        for q, part, src in srcs:
+            n = done("v", vec.tensor_scalar(part, src, HA[q], HB[q], A.mult, A.add))
+        need(vec, "v", "v", n)
+        need(vec, "v", "v", done("v", vec.tensor_scalar(y, x, 5, K - 1, A.arith_shift_right, A.bitwise_and)))
+        return done("v", vec.tensor_copy(off, y))
 
-    def hash_steps(src, x, y, off, a, b):
-        return [lambda: vec.tensor_scalar(x[:, a:b], src[:, a:b], HA[r], HB[r], A.mult, A.add),
-                lambda: vec.tensor_scalar(y[:, a:b], x[:, a:b], 5, K - 1, A.arith_shift_right, A.bitwise_and),
-                lambda: vec.tensor_copy(off[:, a:b], y[:, a:b])]
-
-    def run(steps, n=0):
-        for step in steps:
-            need(vec, "v", "v", n)
-            n = done("v", step())
+    def addresses(a, b):
+        srcs = []
+        for i in range(a, b):
+            q = order[i]
+            if q != r and mine[q][0] > mine[q][1]:
+                srcs += [(q, T.ox[:, i, 0:LH], T.ids8[:, LH:2 * LH]), (q, T.ox[:, i, LH:2 * LH], T.ids8[:, 0:LH])]
+            else:
+                srcs.append((q, T.ox[:, i, :], T.ids8[:, :]))
+        n = hashes(srcs, T.ox[:, a:b, :], T.oy[:, a:b, :], T.oo[:, a:b, :])
+        g.wait_ge(T.sem.v, n)
+        for i in range(a, min(b, N - 2)):
+            c = LH * min(mine[order[i]])
+            rid, pid, _ = topo.addr(T.cores[order[i]])
+            g.remote_dma(T.lo[:, c:c + 2 * LH], T.oo[:, i, :], T.sem["lists%d" % (i // 2)], T.sem.sent, pid, rid, mask)
+            state["sent"] += each
         return n
 
     def pick(eng, me, h, n, off, t, n_off):
@@ -236,125 +333,95 @@ def owner_program(g, core, r, T, topo):
         need(vec, "v", "s", u["s"])
         return done("v", vec.quantize_mx(u["c"], u["p"], u["h"][:, 0:4 * u["n"]]))
 
+    def own_half(half):
+        a = column(r, half)
+        own = {"h": T["ho%d" % half], "n": H, "c": T.rc[:, a:a + H], "p": T.rs[:, a:a + H]}
+        off = T.oo[:, N - 2, LH * half:LH * half + LH]
+        for t in (0, 1):
+            own["s"] = pick(sca, "s", own["h"], H, off, t, n_oo)
+        for t in (2, 3):
+            own["v"] = pick(vec, "v", own["h"], H, off, t, n_oo)
+        return pack(own)
+
     vec.wait_ge(T.sem.idl, 128)
-    n_oo = run(hash_steps(T.ids8, T.ox, T.oy, T.oo, 0, 16))
-    own = {"h": T.ho, "n": TOK, "c": T.rc[:, TOK * r:TOK * r + TOK], "p": T.rs[:, TOK * r:TOK * r + TOK]}
+    order.append(r)
+    addresses(0, 2)
+    n_oo = addresses(2, N - 1)
     planes_ = {}
     sca.wait_ge(T.sem.tbl, 16)
-    planes_[0] = ("s", done("s", sca.activation(T.tp0[:, :], T.tbl[:, 0:4 * K:4], COPY)))
-    vec.wait_ge(T.sem.tbl, 16)
-    for t in (1, 2, 3):
-        planes_[t] = ("v", done("v", vec.tensor_copy(T["tp%d" % t][:, :], T.tbl[:, t:4 * K:4])))
     for t in (0, 1):
-        own["s"] = pick(sca, "s", own["h"], TOK, T.oo[:, 0:16], t, n_oo)
+        planes_[t] = ("s", done("s", sca.activation(T["tp%d" % t][:, :], T.tbl[:, t:4 * K:4], COPY)))
+    vec.wait_ge(T.sem.tbl, 16)
     for t in (2, 3):
-        own["v"] = pick(vec, "v", own["h"], TOK, T.oo[:, 0:16], t, n_oo)
-    n_own = pack(own)
+        planes_[t] = ("v", done("v", vec.tensor_copy(T["tp%d" % t][:, :], T.tbl[:, t:4 * K:4])))
+    g.wait_ge(T.sem.v, own_half(0))
+    to0, a0 = summer(r, 0, T, topo), column(r, 0)
+    state["sent"] += send_pair(g, T, topo, to0, topo.mask(core, to0) & ~mask, T.sem["arr0_%d" % r], T.sem["arr0_%d" % r],
+                               T.rc[:, a0:a0 + H], T.rc[:, a0:a0 + H], T.rs[:, a0:a0 + H], T.rs[:, a0:a0 + H])
 
     def pack_and_send(u):
         g.wait_ge(T.sem.v, pack(u))
         codes, planes = [], []
         for p in u["pieces"]:
-            a, c = column(r, p["half"]), p["col"]
+            a, c, w = column(r, p["half"]), p["col"], p["cols"]
+            if not w:
+                continue
             if p["via"] is None:
-                dst, oc, op = T.cores[p["to"]], T.rc[:, a:a + H], T.rs[:, a:a + H]
+                dst, oc, op = summer(p["to"], p["half"], T, topo), T.rc[:, a:a + w], T.rs[:, a:a + w]
                 sc = sp = T.sem["arr%d_%d" % (p["half"], r)]
             else:
                 b = H * p["place"]
-                dst, oc, op = p["via"], T.hc[:, b:b + H], T.hs[:, b:b + H]
-                sc, sp = T.sem["hcode%d" % p["place"]], T.sem["hplane%d" % p["place"]]
+                dst, oc, op = p["via"], T.hc[:, b:b + w], T.hs[:, b:b + w]
+                sc, sp = T.sem["hcode%d" % p["head"]], T.sem["hplane%d" % p["head"]]
             rid, pid, _ = topo.addr(dst)
             to = [DstId(rid=rid, pnc=pid)]
-            codes.append(RemoteDMATransfer(dst_ids=to, dma_engine_mask=p["mask"], remote_sem=sc, srcs=[u["qc"][:, c:c + H].bitcast(dt.uint8)], dsts=[oc.bitcast(dt.uint8)]))
-            planes.append(RemoteDMATransfer(dst_ids=to, dma_engine_mask=p["mask"], remote_sem=sp, srcs=[u["qs"][:, c:c + H]], dsts=[op]))
+            codes.append(RemoteDMATransfer(dst_ids=to, dma_engine_mask=p["mask"], remote_sem=sc, srcs=[u["qc"][:, c:c + w].bitcast(dt.uint8)], dsts=[oc.bitcast(dt.uint8)]))
+            planes.append(RemoteDMATransfer(dst_ids=to, dma_engine_mask=p["mask"], remote_sem=sp, srcs=[u["qs"][:, c:c + w]], dsts=[op]))
             state["sent"] += 2 * bits(p["mask"])
         g.remote_dma_fused(codes, local_sem=T.sem.sent)
         g.remote_dma_fused(planes, local_sem=T.sem.sent)
 
-    n_of = {}
-
-    def listed(k):
-        a, b = GROUPS[k]
-        vec.wait_ge(T.sem["lists%d" % k], each * (b - a))
-        return hash_steps(T.lst, T.lx, T.ly, T.lo, LH * a, LH * b)
-
-    def known(k, n):
-        for i in range(*GROUPS[k]):
-            n_of[i] = n
-
-    known(0, run(listed(0)))
+    vec.wait_ge(T.sem.raw, each)
+    a = LH * LAYOUT.index((RAW, 0))
+    n_raw = hashes([(r, T.lx[:, :], T.lst[:, :])], T.lx[:, :], T.ly[:, :], T.lo[:, a:a + 2 * LH])
     before = None
     for i, pieces in enumerate(units):
         n = H * len(pieces)
         u = {"h": T["h%d" % i], "n": n, "qc": T["qc%d" % i], "qs": T["qs%d" % i], "c": T["qc%d" % i][:, 0:n], "p": T["qs%d" % i][:, 0:n], "pieces": pieces}
         s = pieces[0]["slot"]
         off = T.lo[:, LH * s:LH * (s + len(pieces))]
-        n_off = n_of[s + len(pieces) - 1]
+        n_off = n_raw if i >= len(LISTS) else 0
+        if i < len(LISTS):
+            sca.wait_ge(T.sem["lists%d" % i], each * LISTS[i])
+            vec.wait_ge(T.sem["lists%d" % i], each * LISTS[i])
         share = UNITS[i][1]
-        steps = listed(2) if i == 1 else []
-        n_h = run(steps[:1])
         for t in range(share):
             u["s"] = pick(sca, "s", u["h"], n, off, t, n_off)
         for t in range(share, 4):
             u["v"] = pick(vec, "v", u["h"], n, off, t, n_off)
-            n_h = run(steps[1 + t - share:2 + t - share], n_h)
             if before is not None:
                 pack_and_send(before)
                 before = None
         before = u
-        if i == 0:
-            known(1, run(listed(1)))
-        if i == 1:
-            known(2, n_h)
     pack_and_send(before)
+    n_own = own_half(1)
 
-    syn.wait_ge(T.sem.lists2, each * (GROUPS[2][1] - GROUPS[2][0]))
+    syn.wait_ge(T.sem["lists%d" % (len(LISTS) - 1)], each * LISTS[-1])
     syn.dma_start(T.ws[:, :], T.w[:, :]).then_inc(T.sem.wl, 16)
     vec.wait_ge(T.sem.wl, 16)
     n_w = done("v", vec.quantize_mx(T.wc[:, 0:128 * O], T.wp[:, 0:128 * O], T.ws[:, 0:512 * O]))
 
-    need(ten, "t", "v", n_e)
-
-    def add(half, k, q):
-        if q == r:
-            need(ten, "t", "v", n_own)
-        else:
-            _, sem, n = arrival(q, r, half, T, topo)
-            ten.wait_ge(T.sem[sem], n)
-        a, n_t = column(q, half), []
-        for b in range(4):
-            c = 512 * (4 * half + b)
-            n_t.append(done("t", ten.matmul_mx(T.ps[:, c:c + H], T.ec[:, 128 * b:128 * b + 128], T.es[:, 128 * b:128 * b + 128],
-                                               T.rc[:, a:a + H], T.rs[:, a:a + H], k == 0, k == N - 1)))
-        return n_t
-
-    def make_v(half, n_t):
-        vt = T["vt%d" % half]
-        for b in range(4):
-            c = 512 * (4 * half + b)
-            o, i = vt[:, b:4 * H:4], T.ps[:, c:c + H]
-            if b % 2 == 0:
-                need(sca, "s", "t", n_t[b])
-                n_s = done("s", sca.activation(o, i, COPY))
-            else:
-                need(vec, "v", "t", n_t[b])
-                n_v = done("v", vec.tensor_copy(o, i))
-        need(vec, "v", "v", n_v)
-        need(vec, "v", "s", n_s)
-        return done("v", vec.quantize_mx(T.vc[:, H * half:H * half + H], T.vs[:, H * half:H * half + H], vt[:, 0:4 * H]))
-
-    def times_w(half, n_q):
+    def times_w(half):
         need(ten, "t", "v", n_w)
-        need(ten, "t", "v", n_q)
         n = []
         for o in range(O):
-            c = 512 * (2 * half + o)
+            c = 512 * (4 + 2 * half + o)
             n.append(done("t", ten.matmul_mx(T.ps[:, c:c + H], T.wc[:, 128 * o:128 * o + 128], T.wp[:, 128 * o:128 * o + 128],
                                              T.vc[:, H * half:H * half + H], T.vs[:, H * half:H * half + H], True, True)))
         return n
 
     def store(half, o, me, n_y, queue, name):
-        y0, c = TOK * o + H * half, 512 * (2 * half + o)
+        y0, c = TOK * o + H * half, 512 * (4 + 2 * half + o)
         eng = sca if me == "s" else vec
         need(eng, me, "t", n_y[o])
         out, in_ = T.yo[:, y0:y0 + H], T.ps[:, c:c + H]
@@ -362,16 +429,14 @@ def owner_program(g, core, r, T, topo):
         need(queue, name, me, n)
         queue.dma_start(T.y[:, y0:y0 + H], T.yo[:, y0:y0 + H]).then_inc(T.sem.yd, 16)
 
-    for k, q in enumerate(chain(r, 0, T, topo)):
-        n_a = add(0, k, q)
-    n_q0 = make_v(0, n_a)
-    for k, q in enumerate(chain(r, 1, T, topo)):
-        n_b = add(1, k, q)
-    n_y0 = times_w(0, n_q0)
+    n_b = add_up(r, 1, lambda: need(ten, "t", "v", n_own))
+    ten.wait_ge(T.sem.v0, 2 * bits(outside(to0, T, topo)))
+    n_y0 = times_w(0)
     n_q1 = make_v(1, n_b)
     for o in range(O):
         store(0, o, "s", n_y0, syn, "y")
-    n_y1 = times_w(1, n_q1)
+    need(ten, "t", "v", n_q1)
+    n_y1 = times_w(1)
     store(1, 0, "s", n_y1, sca, "s")
     store(1, 1, "v", n_y1, syn, "y")
     syn.wait_ge(T.sem.yd, 64)

from concourse.bass import DstId, RemoteDMATransfer
from concourse.mybir import dt, AluOpType, ActivationFunctionType

N, TOK, K, O = 8, 256, 256, 2
H = TOK // 2
HA = (1237, 1811, 947, 1543, 2017, 733, 1409, 1699)
HB = (40503, 12289, 58111, 3571, 27644, 61007, 19211, 50021)
UNITS = (
    ((("p0", 0, "n0"), ("f0", 0, "x0")), 2),
    ((("p1", 0, ""), ("f1", 0, "x1")), 3),
    ((("f2", 0, "x0"), ("p2", 0, "")), 2),
    ((("f0", 1, "x0"), ("m0", 0, "")), 2),
    ((("f1", 1, "x1"), ("f2", 1, "x0")), 2),
    ((("p0", 1, "n0"),), 3),
    ((("p1", 1, ""),), 2),
    ((("p2", 1, ""),), 3),
    ((("m0", 1, ""),), 2),
)
LAYOUT = (("m0", 0), ("m0", 1), ("p1", 1), ("p1", 0), ("f1", 0), ("f1", 1), ("f2", 1), ("f2", 0), ("p2", 0), ("p2", 1))
LAYOUT = (("p0", 1), ("p0", 0), ("f0", 0), ("f0", 1)) + LAYOUT
RAW = "m0"
LISTS = (2, 2, 2)
SLOTS = 2 * (N - 1)
LH = H // 16
PLACES = 4

SCRATCH = {
    "ids8": ("sbuf", [128, 16], "int32"),
    "ox": ("sbuf", [128, N - 1, 2 * LH], "int32"),
    "oy": ("sbuf", [128, N - 1, 2 * LH], "int32"),
    "oo": ("sbuf", [128, N - 1, 2 * LH], "uint16"),
    "lst": ("sbuf", [128, 2 * LH], "int32"),
    "lx": ("sbuf", [128, 2 * LH], "int32"),
    "ly": ("sbuf", [128, 2 * LH], "int32"),
    "lo": ("sbuf", [128, LH * SLOTS], "uint16"),
    "tbl": ("sbuf", [128, 4 * K], "bfloat16"),
    "ws": ("sbuf", [128, 512 * O], "bfloat16"),
    "ones": ("sbuf", [128, 128], "bfloat16"),
    "eye": ("sbuf", [128, 128], "bfloat16"),
    "ez": ("sbuf", [128, 520], "bfloat16"),
    "ec": ("sbuf", [128, 512], "float8_e4m3fn_x4"),
    "es": ("sbuf", [128, 512], "uint8"),
    "wc": ("sbuf", [128, 128 * O], "float8_e4m3fn_x4"),
    "wp": ("sbuf", [128, 128 * O], "uint8"),
    "rc": ("sbuf", [128, N * TOK], "float8_e4m3fn_x4"),
    "rs": ("sbuf", [128, N * TOK], "uint8"),
    "hc": ("sbuf", [128, PLACES * H], "float8_e4m3fn_x4"),
    "hs": ("sbuf", [128, PLACES * H], "uint8"),
    "ho0": ("sbuf", [128, 4 * H], "bfloat16"),
    "ho1": ("sbuf", [128, 4 * H], "bfloat16"),
    "vt": ("sbuf", [128, 4 * H], "bfloat16"),
    "vc": ("sbuf", [128, TOK], "float8_e4m3fn_x4"),
    "vs": ("sbuf", [128, TOK], "uint8"),
    "yo": ("sbuf", [128, O * TOK], "float32"),
    "ps": ("psum", [128, 512 * 8], "float32"),
}
for _i in range(4):
    SCRATCH["tp%d" % _i] = ("sbuf", [128, K], "bfloat16")
for _i, (_u, _s) in enumerate(UNITS):
    SCRATCH["h%d" % _i] = ("sbuf", [128, 4 * H * len(_u)], "bfloat16")
    SCRATCH["qc%d" % _i] = ("sbuf", [128, H * len(_u)], "float8_e4m3fn_x4")
    SCRATCH["qs%d" % _i] = ("sbuf", [128, H * len(_u)], "uint8")

SEMAPHORES = ["idl", "tbl", "wl", "v", "s", "t", "ga", "v0", "raw", "sent", "yd"]
SEMAPHORES += ["lists%d" % i for i in range(len(LISTS))]
SEMAPHORES += ["hcode%d" % i for i in range(PLACES)] + ["hplane%d" % i for i in range(PLACES)]
SEMAPHORES += ["arr%d_%d" % (h, q) for h in range(2) for q in range(N)]


def bits(m):
    return bin(m).count("1")


def as_mask(engines):
    return sum(1 << e for e in engines)


def plan(core, T, topo):
    ch = topo.chip(core)
    r = T.rank_of(core)
    ring = [(r + k) % N for k in range(1, N)]
    who = {"m": [d for d in ring if topo.mates(ch, topo.chip(T.cores[d]))],
           "p": [d for d in ring if topo.same_plane(ch, topo.chip(T.cores[d]))]}
    who["f"] = [d for d in ring if d not in who["m"] and d not in who["p"]]
    who["x"] = [c for c in topo.cores_of(core)
                if topo.die(c) != topo.die(core) and all(topo.may_write(c, T.cores[d]) for d in who["f"])]
    who["n"] = [c for c in topo.cores_of(core) if topo.die(c) == topo.die(core) and c != core]
    off = sorted({e for d in ring for e in topo.engines(core, T.cores[d])})
    every = topo.engines(core, who["n"][0])
    inner = [e for e in every if e not in off]
    used = {}
    units, slot, turn = [], {}, 0
    for u, _ in UNITS:
        pieces = []
        turn += H * len(u)
        for i, (to, half, way) in enumerate(u):
            d = who[to[0]][int(to[1])]
            via = who[way[0]][int(way[1])] if way else None
            slot[(d, half)] = LAYOUT.index((to, half))
            p = {"to": d, "half": half, "slot": slot[(d, half)], "col": i * H, "cols": H, "via": via, "turn": turn}
            if via is not None:
                p["place"] = p["head"] = used.get(via, 0)
                used[via] = p["place"] + 1
            pieces.append(p)
        relayed = [p for p in pieces if p["via"] is not None]
        direct = [p for p in pieces if p["via"] is None]
        if len(relayed) > 1 and len({p["via"] for p in pieces}) == 1:
            for p in pieces:
                p.update(mask=as_mask(every), head=pieces[0]["place"], cols=H * len(u) if p is pieces[0] else 0)
        else:
            rest = relayed[1:] + direct
            for p in relayed[:1]:
                p["mask"] = as_mask(inner)
            for i, p in enumerate(rest):
                w = len(off) // len(rest)
                p["mask"] = as_mask(off[i * w:i * w + w])
        units.append(pieces)
    return units, slot


def places(slot):
    out = {}
    for d, half in sorted(slot, key=slot.get):
        out.setdefault(d, len(out))
    return out


def runs(slot, lo, hi):
    at = places(slot)
    todo = [(s, 2 * at[d] + half) for (d, half), s in sorted(slot.items(), key=lambda x: x[1]) if lo <= at[d] < hi]
    out, i = [], 0
    while i < len(todo):
        s, a = todo[i]
        step = max(todo[i + 1][1] - a, 1) if i + 1 < len(todo) else 1
        n = 1
        while i + n < len(todo) and todo[i + n] == (s + n, a + n * step):
            n += 1
        out.append((s, range(a, a + (n - 1) * step + 1, step)))
        i += n
    return out


def column(q, half):
    return TOK * q + H * half


def summer(r, half, T, topo):
    core = T.cores[r]
    return core if half else [c for c in topo.cores_of(core) if topo.die(c) == topo.die(core) and c != core][0]


def outside(src, T, topo):
    return [topo.mask(src, c) for c in T.cores if topo.chip(c) != topo.chip(src) and topo.may_write(src, c)][0]


def arrival(q, r, half, T, topo):
    for u in plan(T.cores[q], T, topo)[0]:
        for p in u:
            if p["to"] == r and p["half"] == half:
                if p["via"] is None:
                    m, hops = p["mask"], 1
                else:
                    m, hops = topo.mask(p["via"], T.cores[r]), 2
                return p["turn"] + 2 * TOK * hops, "arr%d_%d" % (half, q), 2 * bits(m)


def chain(r, half, T, topo):
    return sorted([0, 1], key=lambda q: 0 if q == r else arrival(q, r, half, T, topo)[0]) + list(range(2, N))


def send_pair(g, T, topo, dst, mask, sem_c, sem_p, oc, ic, op, ip):
    rid, pid, _ = topo.addr(dst)
    g.remote_dma(oc.bitcast(dt.uint8), ic.bitcast(dt.uint8), sem_c, T.sem.sent, pid, rid, mask)
    g.remote_dma(op, ip, sem_p, T.sem.sent, pid, rid, mask)
    return 2 * bits(mask)


def rank_program(g, core, T, topo):
    rank = T.rank_of(core)
    if rank is None:
        helper_program(g, core, T, topo)
        return
    owner_program(g, core, rank, T, topo)


def compute(g, T, topo):
    vec, sca, ten = g.vector, g.scalar, g.tensor
    A = AluOpType
    COPY = ActivationFunctionType.Copy
    cnt = {"v": 0, "s": 0, "t": 0}
    seen = {}

    def done(name, ins):
        ins.then_inc(T.sem[name], 1)
        cnt[name] += 1
        return cnt[name]

    def need(queue, me, name, val):
        if val > seen.get((me, name), 0):
            queue.wait_ge(T.sem[name], val)
            seen[(me, name)] = val

    def constants():
        n_ones = done("v", vec.memset(T.ones[:, :], 1.0))
        n_z = done("v", vec.memset(T.ez[:, :], 0.0))
        g.wait_ge(T.sem.v, n_ones)
        g.affine_select(T.eye[:, :], T.ones[:, :], [[-1, 128]], A.is_equal, 0.0, 0, 1).then_inc(T.sem.ga, 1)
        vec.wait_ge(T.sem.ga, 1)
        need(vec, "v", "v", n_z)
        need(vec, "v", "v", done("v", vec.tensor_copy(T.ez[:, 4:516:4], T.eye[:, :])))
        for b in range(4):
            n_e = done("v", vec.quantize_mx(T.ec[:, 128 * b:128 * b + 128], T.es[:, 128 * b:128 * b + 128], T.ez[:, 4 - b:4 - b + 512]))
        need(ten, "t", "v", n_e)

    def add_up(r, half, own):
        for k, q in enumerate(chain(r, half, T, topo)):
            if q == r:
                own()
            else:
                _, sem, n = arrival(q, r, half, T, topo)
                ten.wait_ge(T.sem[sem], n)
            a, n_t = column(q, half), []
            for b in range(4):
                n_t.append(done("t", ten.matmul_mx(T.ps[:, 512 * b:512 * b + H], T.ec[:, 128 * b:128 * b + 128], T.es[:, 128 * b:128 * b + 128],
                                                   T.rc[:, a:a + H], T.rs[:, a:a + H], k == 0, k == N - 1)))
        return n_t

    def make_v(half, n_t):
        for b in range(4):
            o, i = T.vt[:, b:4 * H:4], T.ps[:, 512 * b:512 * b + H]
            if b % 2 == 0:
                need(sca, "s", "t", n_t[b])
                n_s = done("s", sca.activation(o, i, COPY))
            else:
                need(vec, "v", "t", n_t[b])
                n_v = done("v", vec.tensor_copy(o, i))
        need(vec, "v", "v", n_v)
        need(vec, "v", "s", n_s)
        return done("v", vec.quantize_mx(T.vc[:, H * half:H * half + H], T.vs[:, H * half:H * half + H], T.vt[:, 0:4 * H]))

    return done, need, constants, add_up, make_v


def helper_program(g, core, T, topo):
    src = [c for c in T.cores if topo.chip(c) == topo.chip(core)][0]
    q = T.rank_of(src)
    adds = summer(q, 0, T, topo) == core
    if adds:
        done, need, constants, add_up, make_v = compute(g, T, topo)
        constants()
        own = topo.mask(src, core) & ~outside(src, T, topo)
        n_v = make_v(0, add_up(q, 0, lambda: g.tensor.wait_ge(T.sem["arr0_%d" % q], 2 * bits(own))))
    total = 0
    for p in [p for u in plan(src, T, topo)[0] for p in u if p["via"] == core]:
        dst = summer(p["to"], p["half"], T, topo)
        rid, pid, _ = topo.addr(dst)
        m = topo.mask(core, dst)
        arr = T.sem["arr%d_%d" % (p["half"], q)]
        a, b = column(q, p["half"]), H * p["place"]
        if p["cols"]:
            g.wait_ge(T.sem["hcode%d" % p["head"]], bits(p["mask"]))
        g.remote_dma(T.rc[:, a:a + H].bitcast(dt.uint8), T.hc[:, b:b + H].bitcast(dt.uint8), arr, T.sem.sent, pid, rid, m)
        if p["cols"]:
            g.wait_ge(T.sem["hplane%d" % p["head"]], bits(p["mask"]))
        g.remote_dma(T.rs[:, a:a + H], T.hs[:, b:b + H], arr, T.sem.sent, pid, rid, m)
        total += 2 * bits(m)
    if adds:
        g.wait_ge(T.sem.v, n_v)
        total += send_pair(g, T, topo, src, topo.mask(core, src) & ~outside(core, T, topo), T.sem.v0, T.sem.v0, T.vc[:, 0:H], T.vc[:, 0:H], T.vs[:, 0:H], T.vs[:, 0:H])
    if total:
        g.wait_ge(T.sem.sent, total)


def owner_program(g, core, r, T, topo):
    vec, sca, ten, syn = g.vector, g.scalar, g.tensor, g.sync
    A = AluOpType
    COPY = ActivationFunctionType.Copy
    done, need, constants, add_up, make_v = compute(g, T, topo)
    units, slot = plan(core, T, topo)
    others = [d for d in range(N) if d != r]
    groups = [(sum(LISTS[:k]), sum(LISTS[:k + 1])) for k in range(len(LISTS))]

    for i in range(8):
        (syn if i < 4 else sca).dma_start(T.ids8[16 * i:16 * i + 16, :], T.ids[:, :]).then_inc(T.sem.idl, 16)
    syn.dma_start(T.tbl[:, :], T.tb[:, :]).then_inc(T.sem.tbl, 16)

    constants()

    g.wait_ge(T.sem.idl, 128)
    mask = outside(core, T, topo)
    each = bits(mask)
    state = {"sent": 0}
    mine = {d: [plan(T.cores[d], T, topo)[1][(r, half)] for half in range(2)] for d in others}
    order = sorted(others, key=mine.get)
    raw = [d for d in order if LAYOUT[mine[d][0]][0] == RAW][0]
    order.remove(raw)
    rid, pid, _ = topo.addr(T.cores[raw])
    g.remote_dma(T.lst[:, :], T.ids8[:, :], T.sem.raw, T.sem.sent, pid, rid, mask)
    state["sent"] += each

    def hashes(srcs, x, y, off):
        for q, part, src in srcs:
            n = done("v", vec.tensor_scalar(part, src, HA[q], HB[q], A.mult, A.add))
        need(vec, "v", "v", n)
        need(vec, "v", "v", done("v", vec.tensor_scalar(y, x, 5, K - 1, A.arith_shift_right, A.bitwise_and)))
        return done("v", vec.tensor_copy(off, y))

    def addresses(a, b):
        srcs = []
        for i in range(a, b):
            q = order[i]
            if q != r and mine[q][0] > mine[q][1]:
                srcs += [(q, T.ox[:, i, 0:LH], T.ids8[:, LH:2 * LH]), (q, T.ox[:, i, LH:2 * LH], T.ids8[:, 0:LH])]
            else:
                srcs.append((q, T.ox[:, i, :], T.ids8[:, :]))
        n = hashes(srcs, T.ox[:, a:b, :], T.oy[:, a:b, :], T.oo[:, a:b, :])
        g.wait_ge(T.sem.v, n)
        for i in range(a, min(b, N - 2)):
            c = LH * min(mine[order[i]])
            rid, pid, _ = topo.addr(T.cores[order[i]])
            g.remote_dma(T.lo[:, c:c + 2 * LH], T.oo[:, i, :], T.sem["lists%d" % (i // 2)], T.sem.sent, pid, rid, mask)
            state["sent"] += each
        return n

    def pick(eng, me, h, n, off, t, n_off):
        need(eng, me, "v", n_off)
        need(eng, me, planes_[t][0], planes_[t][1])
        o, i = h[:, t:4 * n:4], T["tp%d" % t][:, 0:K].indirect(off)
        return done(me, sca.activation(o, i, COPY) if me == "s" else vec.tensor_copy(o, i))

    def pack(u):
        need(vec, "v", "v", u["v"])
        need(vec, "v", "s", u["s"])
        return done("v", vec.quantize_mx(u["c"], u["p"], u["h"][:, 0:4 * u["n"]]))

    def own_half(half):
        a = column(r, half)
        own = {"h": T["ho%d" % half], "n": H, "c": T.rc[:, a:a + H], "p": T.rs[:, a:a + H]}
        off = T.oo[:, N - 2, LH * half:LH * half + LH]
        for t in (0, 1):
            own["s"] = pick(sca, "s", own["h"], H, off, t, n_oo)
        for t in (2, 3):
            own["v"] = pick(vec, "v", own["h"], H, off, t, n_oo)
        return pack(own)

    vec.wait_ge(T.sem.idl, 128)
    order.append(r)
    addresses(0, 2)
    n_oo = addresses(2, N - 1)
    planes_ = {}
    sca.wait_ge(T.sem.tbl, 16)
    for t in (0, 1):
        planes_[t] = ("s", done("s", sca.activation(T["tp%d" % t][:, :], T.tbl[:, t:4 * K:4], COPY)))
    vec.wait_ge(T.sem.tbl, 16)
    for t in (2, 3):
        planes_[t] = ("v", done("v", vec.tensor_copy(T["tp%d" % t][:, :], T.tbl[:, t:4 * K:4])))
    g.wait_ge(T.sem.v, own_half(0))
    to0, a0 = summer(r, 0, T, topo), column(r, 0)
    state["sent"] += send_pair(g, T, topo, to0, topo.mask(core, to0) & ~mask, T.sem["arr0_%d" % r], T.sem["arr0_%d" % r],
                               T.rc[:, a0:a0 + H], T.rc[:, a0:a0 + H], T.rs[:, a0:a0 + H], T.rs[:, a0:a0 + H])

    def pack_and_send(u):
        g.wait_ge(T.sem.v, pack(u))
        codes, planes = [], []
        for p in u["pieces"]:
            a, c, w = column(r, p["half"]), p["col"], p["cols"]
            if not w:
                continue
            if p["via"] is None:
                dst, oc, op = summer(p["to"], p["half"], T, topo), T.rc[:, a:a + w], T.rs[:, a:a + w]
                sc = sp = T.sem["arr%d_%d" % (p["half"], r)]
            else:
                b = H * p["place"]
                dst, oc, op = p["via"], T.hc[:, b:b + w], T.hs[:, b:b + w]
                sc, sp = T.sem["hcode%d" % p["head"]], T.sem["hplane%d" % p["head"]]
            rid, pid, _ = topo.addr(dst)
            to = [DstId(rid=rid, pnc=pid)]
            codes.append(RemoteDMATransfer(dst_ids=to, dma_engine_mask=p["mask"], remote_sem=sc, srcs=[u["qc"][:, c:c + w].bitcast(dt.uint8)], dsts=[oc.bitcast(dt.uint8)]))
            planes.append(RemoteDMATransfer(dst_ids=to, dma_engine_mask=p["mask"], remote_sem=sp, srcs=[u["qs"][:, c:c + w]], dsts=[op]))
            state["sent"] += 2 * bits(p["mask"])
        g.remote_dma_fused(codes, local_sem=T.sem.sent)
        g.remote_dma_fused(planes, local_sem=T.sem.sent)

    vec.wait_ge(T.sem.raw, each)
    a = LH * LAYOUT.index((RAW, 0))
    n_raw = hashes([(r, T.lx[:, :], T.lst[:, :])], T.lx[:, :], T.ly[:, :], T.lo[:, a:a + 2 * LH])
    before = None
    for i, pieces in enumerate(units):
        n = H * len(pieces)
        u = {"h": T["h%d" % i], "n": n, "qc": T["qc%d" % i], "qs": T["qs%d" % i], "c": T["qc%d" % i][:, 0:n], "p": T["qs%d" % i][:, 0:n], "pieces": pieces}
        s = pieces[0]["slot"]
        off = T.lo[:, LH * s:LH * (s + len(pieces))]
        n_off = n_raw if i >= len(LISTS) else 0
        if i < len(LISTS):
            sca.wait_ge(T.sem["lists%d" % i], each * LISTS[i])
            vec.wait_ge(T.sem["lists%d" % i], each * LISTS[i])
        share = UNITS[i][1]
        for t in range(share):
            u["s"] = pick(sca, "s", u["h"], n, off, t, n_off)
        for t in range(share, 4):
            u["v"] = pick(vec, "v", u["h"], n, off, t, n_off)
            if before is not None:
                pack_and_send(before)
                before = None
        before = u
    pack_and_send(before)
    n_own = own_half(1)

    syn.wait_ge(T.sem["lists%d" % (len(LISTS) - 1)], each * LISTS[-1])
    syn.dma_start(T.ws[:, :], T.w[:, :]).then_inc(T.sem.wl, 16)
    vec.wait_ge(T.sem.wl, 16)
    n_w = done("v", vec.quantize_mx(T.wc[:, 0:128 * O], T.wp[:, 0:128 * O], T.ws[:, 0:512 * O]))

    def times_w(half):
        need(ten, "t", "v", n_w)
        n = []
        for o in range(O):
            c = 512 * (4 + 2 * half + o)
            n.append(done("t", ten.matmul_mx(T.ps[:, c:c + H], T.wc[:, 128 * o:128 * o + 128], T.wp[:, 128 * o:128 * o + 128],
                                             T.vc[:, H * half:H * half + H], T.vs[:, H * half:H * half + H], True, True)))
        return n

    def store(half, o, me, n_y, queue, name):
        y0, c = TOK * o + H * half, 512 * (4 + 2 * half + o)
        eng = sca if me == "s" else vec
        need(eng, me, "t", n_y[o])
        out, in_ = T.yo[:, y0:y0 + H], T.ps[:, c:c + H]
        n = done(me, sca.activation(out, in_, COPY) if me == "s" else vec.tensor_copy(out, in_))
        need(queue, name, me, n)
        queue.dma_start(T.y[:, y0:y0 + H], T.yo[:, y0:y0 + H]).then_inc(T.sem.yd, 16)

    n_b = add_up(r, 1, lambda: need(ten, "t", "v", n_own))
    ten.wait_ge(T.sem.v0, 2 * bits(outside(to0, T, topo)))
    n_y0 = times_w(0)
    n_q1 = make_v(1, n_b)
    for o in range(O):
        store(0, o, "s", n_y0, syn, "y")
    need(ten, "t", "v", n_q1)
    n_y1 = times_w(1)
    store(1, 0, "s", n_y1, sca, "s")
    store(1, 1, "v", n_y1, syn, "y")
    syn.wait_ge(T.sem.yd, 64)
    g.wait_ge(T.sem.sent, state["sent"])
